import numpy as np
import ml_dtypes


def mxq(x, axis, fmt="e4m3"):
    dtype, down = {"e4m3": (ml_dtypes.float8_e4m3fn, 7), "e5m2": (ml_dtypes.float8_e5m2, 14)}[fmt]
    v = np.moveaxis(np.asarray(x, np.float32).astype(ml_dtypes.bfloat16).astype(np.float64), axis, -1)
    blocks = v.reshape(v.shape[:-1] + (-1, 32))
    amax = np.abs(blocks).max(-1, keepdims=True)
    byte = np.maximum(np.where(amax > 0, np.frexp(amax)[1] - 1 + 127, 0) - down, 1)
    scale = np.exp2(byte - 127.0)
    codes = (blocks / scale).astype(np.float32).astype(dtype).astype(np.float64)
    return np.moveaxis((codes * scale).reshape(v.shape), -1, axis)


WIDE = False


def mx_kscale(k):
    if not WIDE:
        return np.ones(k)
    levels = np.array([10, -10, 5, -5, 0])
    if k % 512:
        return np.exp2(np.random.permutation(np.resize(levels, k // 32))).repeat(32)
    a = np.empty((k // 512, 16))
    for p in range(k // 512):
        a[p, :8] = np.random.permutation(np.resize(levels, 8))
        for g in range(8):
            far = levels[np.abs(levels - a[p, g]) >= 10]
            a[p, g + 8] = far[np.random.randint(len(far))]
    return np.exp2(a.ravel()).repeat(32)


def f64(x):
    return np.asarray(x).astype(np.float64)


def striped(idx):
    return np.tile(idx.reshape(-1, 16).T, (8, 1)).astype(np.uint16)


def unstriped(offs):
    return offs[:16].T.reshape(-1).astype(np.int64)


E2M1 = np.array([0.0, 0.5, 1.0, 1.5, 2.0, 3.0, 4.0, 6.0, -0.0, -0.5, -1.0, -1.5, -2.0, -3.0, -4.0, -6.0])


def pack_weight(w, fmt):
    k, n = w.shape
    w = f64(np.asarray(w, np.float32).astype(ml_dtypes.bfloat16)).reshape(k // 32, 32, n)
    amax = np.abs(w).max(1)
    if fmt == "e4m3":
        byte = np.frexp(amax)[1] - 1 + 127 - 7
    else:
        mant, ex = np.frexp(amax / 6.0)
        byte = np.where(mant > 0.5, ex, ex - 1) + 127
    byte = np.clip(np.where(amax > 0, byte, 1), 1, 254)
    scaled = (w * np.exp2(127.0 - byte)[:, None, :]).reshape(k, n).astype(np.float32)
    by_word = np.ascontiguousarray(scaled.reshape(k // 512, 128, 4, n).transpose(0, 1, 3, 2))
    if fmt == "e4m3":
        words = by_word.astype(ml_dtypes.float8_e4m3fn).view(np.uint8)
    else:
        c = by_word.astype(ml_dtypes.float4_e2m1fn).view(np.uint8) & 0xF
        words = (c[..., 0::2] | (c[..., 1::2] << 4)).reshape(k // 512, 128, 2 * n)
    return np.ascontiguousarray(words), np.ascontiguousarray(byte.astype(np.uint8).reshape(k // 512, 16, n))


def unpack_weight(words, scales, fmt):
    g, _, n = scales.shape
    words = np.ascontiguousarray(words).reshape(g, 128, n, -1)
    if fmt == "e4m3":
        vals = words.view(ml_dtypes.float8_e4m3fn).astype(np.float64)
    else:
        nib = np.empty((g, 128, n, 4), np.uint8)
        nib[..., 0::2] = words & 0xF
        nib[..., 1::2] = words >> 4
        vals = E2M1[nib]
    vals = vals * np.repeat(np.exp2(scales.astype(np.float64) - 127.0), 8, axis=1)[..., None]
    return vals.transpose(0, 1, 3, 2).reshape(g * 512, n)


def gelu(v):
    return 0.5 * v * (1.0 + np.tanh(np.sqrt(2.0 / np.pi) * (v + 0.044715 * v**3)))


def bf(x):
    return np.asarray(x, np.float32).astype(ml_dtypes.bfloat16)


def planes(Y):
    n, m = Y.shape
    b = f64(bf(Y)).reshape(n // 32, 32, m)
    amax = np.abs(b).max(1)
    byte = np.clip(np.where(amax > 0, np.frexp(amax)[1] - 1 + 127 - 7, 1), 1, 254)
    codes = (b * np.exp2(127.0 - byte)[:, None, :]).reshape(n, m).astype(np.float32).astype(ml_dtypes.float8_e4m3fn).view(np.uint8)
    words = codes.reshape(n // 512, 128, 4, m).transpose(0, 1, 3, 2)
    return np.ascontiguousarray(words), np.ascontiguousarray(byte.astype(np.uint8).reshape(n // 512, 16, m))


K, H, N, T, S, T2, P = 1024, 1024, 384, 2048, 1024, 2048, 512

def setup_inputs():
    n = np.random.standard_normal
    s = mx_kscale(K)[:, None]
    u = mx_kscale(H)[:, None]
    d = {}
    d["tab_words"], d["tab_scales"] = pack_weight(n((K, T)) * s, "e4m3")
    d["offs"] = striped(np.random.permutation(T)[:S])
    d["offs2"] = striped(np.random.permutation(T2)[:S])
    d["offs3"] = striped(np.random.permutation(T2)[:P])
    d["w1"] = (n((K, H)) / K ** 0.5 / s).astype(np.float32)
    d["w2_words"], d["w2_scales"] = pack_weight(n((K, H)) / K ** 0.5 / s, "e2m1")
    d["gain"] = (np.exp(0.3 * n(H)) * u[:, 0]).astype(np.float32)
    d["wgs"] = np.exp(0.3 * n((128, S))).astype(np.float32)
    d["page0"] = (n((H, T2)) * u).astype(np.float32)
    d["sv"] = np.exp(0.4 * n(H)).astype(np.float32)
    d["w3"] = (n((H, N)) / H ** 0.5 / u).astype(np.float32)
    return d

def reference(tab_words, tab_scales, offs, offs2, offs3, w1, w2_words, w2_scales, gain, wgs, page0, sv, w3):
    v = unpack_weight(tab_words, tab_scales, "e4m3")[:, unstriped(offs)]
    w2 = unpack_weight(w2_words, w2_scales, "e2m1")
    a = mxq(f64(w1), 0, "e4m3").T @ v
    b = w2.T @ v
    h = f64(gain)[:, None] * (np.abs(a) - np.abs(b))
    page = f64(page0).copy()
    page[:, unstriped(offs2)] = np.tile(f64(wgs), (H // 128, 1)) * h
    x = f64(sv)[:, None] * page[:, unstriped(offs3)]
    y = np.square(mxq(f64(w3), 0, "e4m3").T @ mxq(x, 0, "e4m3"))
    words, scales = planes(page)
    return y, page, words, scales

@@ -1,0 +1,397 @@
+from contextlib import ExitStack
+
+import concourse.mybir as mybir
+from concourse.masks import make_identity
+
+K, H, N, T, S, T2, M = 1024, 1024, 384, 2048, 1024, 2048, 512
+FLOPS = 2 * 2 * K * H * S + 2 * H * N * M
+
+F32 = mybir.dt.float32
+BF16 = mybir.dt.bfloat16
+I32 = mybir.dt.int32
+U32 = mybir.dt.uint32
+U16 = mybir.dt.uint16
+U8 = mybir.dt.uint8
+FP8X4 = mybir.dt.float8_e4m3fn_x4
+FP4X4 = mybir.dt.float4_e2m1fn_x4
+ACT = mybir.ActivationFunctionType
+MULT = mybir.AluOpType.mult
+
+P = 128
+PACK = 4
+PASS = P * PACK
+BANK = 512
+QUARTER = 256
+
+
+def tile_list_linen_soil_slots_kernel(
+    tc, tab_words, tab_scales, offs, offs2, offs3, w1, w2_words, w2_scales, gain, wgs, page0, sv, w3,
+    out_0, out_1, out_2, out_3,
+):
+    nc = tc.nc
+    with ExitStack() as ctx:
+        keep = ctx.enter_context(tc.tile_pool(name="keep", bufs=1))
+        ring = ctx.enter_context(tc.tile_pool(name="ring", bufs=1))
+        psum = ctx.enter_context(tc.psum_pool(name="psum", bufs=1))
+
+        def wide(shape, dtype, name):
+            return ring.tile(shape, dtype, name=name, tag="wide", bufs=4, align_bytes=64)
+
+        def half(shape, name):
+            return ring.tile(shape, BF16, name=name, tag="half", bufs=2, align_bytes=64)
+
+        def late(shape, dtype, name):
+            return ring.tile(shape, dtype, name=name, tag="late", bufs=4, align_bytes=64)
+
+        def interleave(engine, dst, src):
+            d = dst.rearrange("p (c i) t -> p c t i", i=4)
+            s = src.rearrange("p t (c i) -> p c t i", i=4)
+            if engine == "scalar":
+                nc.scalar.copy(out=d, in_=s)
+            else:
+                nc.vector.tensor_copy(out=d, in_=s)
+
+        def scale_rows(queue, plane, scales):
+            for q in range(4):
+                queue.dma_start(
+                    out=plane[32 * q : 32 * q + 4, :].bitcast(I32).rearrange("p (a c) -> p a c", a=2),
+                    in_=scales[:, 4 * q : 4 * q + 4, :].rearrange("a r c -> r a c").bitcast(I32),
+                )
+
+        list1 = keep.tile([P, S // 16], U16, name="list1")
+        list2 = keep.tile([P, S // 16], U16, name="list2")
+        list3 = keep.tile([P, M // 16], U16, name="list3")
+        tab_plane = keep.tile([P, 2 * T], U8, name="tab_plane", align_bytes=64)
+        w2_plane = keep.tile([P, 2 * H], U8, name="w2_plane", align_bytes=64)
+        nc.vector.memset(tab_plane[:].bitcast(I32), 0)
+        nc.gpsimd.memset(w2_plane[:].bitcast(I32), 0)
+        scale_rows(nc.gpsimd, w2_plane, w2_scales)
+        ident = keep.tile([P, P], F32, name="ident")
+        make_identity(nc, ident[:])
+        gains = keep.tile([P, 2, PACK], F32, name="gains")
+        svs = keep.tile([P, 2, PACK], F32, name="svs")
+        nc.gpsimd.dma_start(out=gains[:], in_=gain.rearrange("(g p t) -> p g t", g=2, t=PACK))
+
+        def load_w1(g, a):
+            raw = wide([P, PACK, BANK], F32, f"w1raw{g}{a}")
+            nc.sync.dma_start(
+                out=raw[:],
+                in_=w1[PASS * a : PASS * (a + 1), PASS * g : PASS * (g + 1)].rearrange("(p i) c -> p i c", i=PACK),
+            )
+            return raw
+
+        def load_tab(a):
+            words = wide([P, T], U32, f"tab{a}")
+            nc.sync.dma_start(out=words[:].bitcast(I32), in_=tab_words[a].rearrange("p t i -> p (t i)").bitcast(I32))
+            return words
+
+        w2_codes = [keep.tile([P, 2, 2 * PASS], U8, name="w2_codes0", align_bytes=64), late([P, 2, 2 * PASS], U8, "w2_codes1")]
+
+        def load_w2(g):
+            nc.sync.dma_start(
+                out=w2_codes[g][:].bitcast(I32),
+                in_=w2_words[:, :, 2 * PASS * g : 2 * PASS * (g + 1)].rearrange("a p c -> p a c").bitcast(I32),
+            )
+
+        weights = keep.tile([P, PACK, S], F32, name="weights")
+
+        def load_weights(j0, j1):
+            for q in (0, 2, 1, 3):
+                nc.sync.dma_start(
+                    out=weights[32 * q : 32 * (q + 1), :, j0:j1],
+                    in_=wgs[:, j0:j1].rearrange("(p t) j -> p t j", t=PACK),
+                )
+
+        pages = {}
+        page_in = page0.rearrange("(g p t) m -> g t p m", g=2, t=PACK)
+        page_out = out_1.rearrange("(g p t) m -> g t p m", g=2, t=PACK)
+
+        def load_page(g, t):
+            pages[g, t] = ring.tile([P, T2], F32, name=f"page{g}{t}", tag="page", bufs=7)
+            nc.sync.dma_start(out=pages[g, t][:], in_=page_in[g, t])
+
+        w1_raw = {(0, 0): load_w1(0, 0)}
+        scale_rows(nc.sync, tab_plane, tab_scales)
+        nc.sync.dma_start(list1[:], offs)
+        w1_raw[0, 1] = load_w1(0, 1)
+        tabs = [load_tab(0)]
+        load_w2(0)
+        tabs.append(load_tab(1))
+        nc.sync.dma_start(list2[:], offs2)
+        load_weights(0, QUARTER)
+        for t in range(PACK):
+            load_page(0, t)
+        load_weights(QUARTER, 2 * QUARTER)
+        w1_raw[1, 0] = load_w1(1, 0)
+        w1_raw[1, 1] = load_w1(1, 1)
+        load_weights(2 * QUARTER, S)
+        load_w2(1)
+        nc.sync.dma_start(list3[:], offs3)
+        nc.sync.dma_start(out=svs[:], in_=sv.rearrange("(g p t) -> p g t", g=2, t=PACK))
+        w3_raw = []
+        for g in range(2):
+            raw = wide([P, PACK, N], F32, f"w3raw{g}")
+            nc.sync.dma_start(out=raw[:], in_=w3[PASS * g : PASS * (g + 1), :].rearrange("(p i) n -> p i n", i=PACK))
+            w3_raw.append(raw)
+        for t in range(3):
+            load_page(1, t)
+
+        v_codes = [late([P, S], U32, f"v_codes{a}") for a in range(2)]
+        v_plane = [keep.tile([P, S], U8, name=f"v_plane{a}", align_bytes=64) for a in range(2)]
+        w1_codes = [keep.tile([P, 2 * BANK], U32, name="w1_codes0", align_bytes=64), late([P, 2 * BANK], U32, "w1_codes1")]
+        w1_plane = keep.tile([P, 4 * BANK], U8, name="w1_plane", align_bytes=64)
+
+        def quantize(codes, plane, grouped):
+            nc.vector.quantize_mx(out=codes.bitcast(FP8X4), scales=plane, in_=grouped)
+
+        def quantize_w1(g, a):
+            if g == 0:
+                grouped = half([P, BANK, PACK], f"w1bf{g}{a}")
+            else:
+                grouped = unit_tile([P, BANK, PACK], BF16, a, 2, f"w1bf{g}{a}")
+            interleave("scalar", grouped[:], w1_raw[g, a][:])
+            cols = slice((2 * g + a) * BANK, (2 * g + a + 1) * BANK)
+            quantize(w1_codes[g][:, a * BANK : (a + 1) * BANK], w1_plane[:, cols], grouped[:].rearrange("p c t -> p (c t)"))
+
+        def gather_words(a, j0, j1):
+            nc.vector.tensor_copy(v_codes[a][:, j0:j1], tabs[a][:].indirect(list1[:, j0 // 16 : j1 // 16]))
+
+        def gather_scales(a, j0, j1):
+            window = tab_plane[:, a * T : (a + 1) * T]
+            nc.vector.tensor_copy(v_plane[a][:, j0:j1], window.indirect(list1[:, j0 // 16 : j1 // 16]))
+
+        for a in range(2):
+            quantize_w1(0, a)
+        for a in range(2):
+            gather_scales(a, 0, S)
+        for j0, j1 in ((0, QUARTER), (QUARTER, S)):
+            for a in range(2):
+                gather_words(a, j0, j1)
+
+        mags = {}
+
+        def bank_tile(shape, n, name):
+            return psum.tile(shape, F32, name=name, tag=f"bank{n}", bufs=1)
+
+        def unit_tile(shape, dtype, side, q, name):
+            return ring.tile(shape, dtype, name=name, tag=f"unit{side}{q}", bufs=1, align_bytes=64)
+
+        def magnitudes(g, jb):
+            if jb % 2 == 0:
+                for side in range(2):
+                    mags[side, jb // 2] = unit_tile([P, 2, PACK, P], F32, side, jb // 2, f"mag{g}{side}{jb // 2}")
+            mag_a = mags[0, jb // 2][:, jb % 2]
+            neg_b = mags[1, jb // 2][:, jb % 2]
+            js = slice(P * jb, P * (jb + 1))
+            acc_a = bank_tile([P, BANK], 4 * g + 2 * (jb % 2), "acc_a")
+            acc_b = bank_tile([P, BANK], 4 * g + 2 * (jb % 2) + 1, "acc_b")
+            for a in range(2):
+                cols = slice((2 * g + a) * BANK, (2 * g + a + 1) * BANK)
+                nc.tensor.matmul_mx(
+                    out=acc_a[:], lhsT=v_codes[a][:, js].bitcast(FP8X4), lhsT_scale=v_plane[a][:, js],
+                    rhs=w1_codes[g][:, a * BANK : (a + 1) * BANK].bitcast(FP8X4), rhs_scale=w1_plane[:, cols], start=(a == 0), stop=(a == 1),
+                )
+            for a in range(2):
+                nc.tensor.matmul_mx(
+                    out=acc_b[:], lhsT=v_codes[a][:, js].bitcast(FP8X4), lhsT_scale=v_plane[a][:, js],
+                    rhs=w2_codes[g][:, a, :].bitcast(FP4X4),
+                    rhs_scale=w2_plane[:, a * H + PASS * g : a * H + PASS * (g + 1)], start=(a == 0), stop=(a == 1),
+                )
+            nc.scalar.activation(out=neg_b, in_=acc_b[:].rearrange("j (p t) -> j t p", t=PACK), func=ACT.Abs)
+            nc.scalar.activation(out=mag_a, in_=acc_a[:].rearrange("j (p t) -> j t p", t=PACK), func=ACT.Abs)
+            nc.scalar.activation(out=neg_b, in_=neg_b, func=ACT.Copy, scale=-1.0)
+
+        def turn(bank, t, jb):
+            nc.tensor.matmul(out=bank, lhsT=mags[0, jb // 2][:, jb % 2, t, :], rhs=ident[:], is_transpose=True, start=True, stop=False)
+            nc.tensor.matmul(out=bank, lhsT=mags[1, jb // 2][:, jb % 2, t, :], rhs=ident[:], is_transpose=True, start=False, stop=True)
+
+        def scatter(g, t, h, j0, j1):
+            nc.vector.tensor_tensor(
+                pages[g, t][:].indirect(list2[:, j0 // 16 : j1 // 16]), h, weights[:, t, j0:j1], MULT
+            )
+
+        def quarter_unit(q):
+            for t in range(PACK):
+                bank = bank_tile([P, QUARTER], 4 + t, "turned")
+                for b in range(2):
+                    turn(bank[:, P * b : P * (b + 1)], t, 2 * q + b)
+                h = ring.tile([P, QUARTER], F32, name="h_quarter", tag="h_quarter", bufs=8)
+                nc.scalar.activation(out=h[:], in_=bank[:], func=ACT.Copy, scale=gains[:, 0, t : t + 1])
+                scatter(0, t, h[:], QUARTER * q, QUARTER * (q + 1))
+
+        h_rows = {}
+
+        def half_row(t, u):
+            if u == 0:
+                h_rows[t] = ring.tile([P, S], F32, name=f"h_row{t}", tag="h_row", bufs=3)
+            bank = bank_tile([P, BANK], (2 * u + t) % 4 if t < 2 else 2 * (t - 2) + u, "turned")
+            for b in range(4):
+                turn(bank[:, P * b : P * (b + 1)], t, 4 * u + b)
+            nc.scalar.activation(
+                out=h_rows[t][:, BANK * u : BANK * (u + 1)], in_=bank[:], func=ACT.Copy, scale=gains[:, 1, t : t + 1]
+            )
+
+        x_codes = [keep.tile([P, M], U32, name=f"x_codes{g}", align_bytes=64) for g in range(2)]
+        x_plane = [keep.tile([P, M], U8, name=f"x_plane{g}", align_bytes=64) for g in range(2)]
+        x_tiles = {}
+        picked = {}
+
+        def fetch(g, t):
+            picked[g, t] = ring.tile([P, M], F32, name="picked", tag="picked", bufs=4)
+            nc.vector.tensor_copy(picked[g, t][:], pages[g, t][:].indirect(list3[:]))
+
+        def scale_x(g, t):
+            if t == 0:
+                x_tiles[g] = late([P, PACK, M], BF16, "x_rows") if g == 0 else late([P, M, PACK], BF16, "xbf1")
+            dst = x_tiles[g][:, t, :] if g == 0 else x_tiles[g][:, :, t]
+            nc.scalar.activation(out=dst, in_=picked[g, t][:], func=ACT.Copy, scale=svs[:, g, t : t + 1])
+
+        def quantize_x(g):
+            grouped = x_tiles[g]
+            if g == 0:
+                grouped = late([P, M, PACK], BF16, "xbf0")
+                interleave("scalar", grouped[:], x_tiles[g][:])
+            quantize(x_codes[g][:], x_plane[g][:], grouped[:].rearrange("p c t -> p (c t)"))
+
+        def store_page(g, t):
+            nc.sync.dma_start(out=page_out[g, t], in_=pages[g, t][:])
+
+        stages = {}
+
+        def regroup(g, t, c, by_vector=False):
+            if (g, c) not in stages:
+                stages[g, c] = wide([P, PACK, BANK], F32, f"stage{g}{c}")
+            src = pages[g, t][:, BANK * c : BANK * (c + 1)]
+            if by_vector:
+                nc.vector.tensor_copy(out=stages[g, c][:, t, :], in_=src)
+            else:
+                nc.sync.dma_start(out=stages[g, c][:, t, :], in_=src)
+
+        y_planes = [keep.tile([P, T2], U8, name=f"y_plane{g}", align_bytes=64) for g in range(2)]
+
+        rounded = {}
+
+        def round_planes(g, c, engine):
+            rounded[g, c] = late([P, BANK, PACK], BF16, f"ybf{g}{c}")
+            interleave(engine, rounded[g, c][:], stages[g, c][:])
+
+        def round_three(c):
+            rounded[1, c] = half([P, BANK, PACK], f"ybf1{c}")
+            interleave("scalar", rounded[1, c][:, :, 0:3], stages[1, c][:, 0:3, :])
+
+        def round_last(c):
+            nc.scalar.copy(out=rounded[1, c][:, :, 3], in_=pages[1, 3][:, BANK * c : BANK * (c + 1)])
+
+        def planes(g, c):
+            cols = slice(BANK * c, BANK * (c + 1))
+            grouped = rounded[g, c]
+            codes = ring.tile([P, BANK], U32, name="y_codes", tag="y_codes", bufs=4, align_bytes=64)
+            quantize(codes[:], y_planes[g][:, cols], grouped[:].rearrange("p c t -> p (c t)"))
+            nc.sync.dma_start(
+                out=out_2[g, :, cols, :].rearrange("p m t -> p (m t)").bitcast(I32), in_=codes[:].bitcast(I32)
+            )
+
+        def store_scales(g):
+            for q in range(4):
+                nc.sync.dma_start(
+                    out=out_3[g, 4 * q : 4 * q + 4, :].bitcast(I32), in_=y_planes[g][32 * q : 32 * q + 4, :].bitcast(I32)
+                )
+
+        w3_codes = keep.tile([P, 2 * N], U32, name="w3_codes", align_bytes=64)
+        w3_plane = keep.tile([P, 2 * N], U8, name="w3_plane", align_bytes=64)
+
+        def quantize_w3(g):
+            grouped = unit_tile([P, N, PACK], BF16, g, 3, f"w3bf{g}")
+            interleave("scalar", grouped[:], w3_raw[g][:])
+            for c0, c1 in ((0, 256), (256, N)):
+                quantize(
+                    w3_codes[:, N * g + c0 : N * g + c1], w3_plane[:, N * g + c0 : N * g + c1],
+                    grouped[:, c0:c1, :].rearrange("p c t -> p (c t)"),
+                )
+
+        scores = {}
+
+        def score_pass(g):
+            for n in range(3):
+                if g == 0:
+                    scores[n] = bank_tile([P, M], 4 + n, f"score{n}")
+                cols = slice(N * g + P * n, N * g + P * (n + 1))
+                nc.tensor.matmul_mx(
+                    out=scores[n][:], lhsT=w3_codes[:, cols].bitcast(FP8X4), lhsT_scale=w3_plane[:, cols],
+                    rhs=x_codes[g][:].bitcast(FP8X4), rhs_scale=x_plane[g][:], start=(g == 0), stop=(g == 1),
+                )
+
+        for q in range(4):
+            if q == 3:
+                quantize_w1(1, 0)
+                quantize_w1(1, 1)
+            magnitudes(0, 2 * q)
+            magnitudes(0, 2 * q + 1)
+            quarter_unit(q)
+        quantize_w3(0)
+        quantize_w3(1)
+        for t in range(PACK):
+            store_page(0, t)
+
+        for u in range(2):
+            for jb in range(4 * u, 4 * u + 4):
+                magnitudes(1, jb)
+            for t in range(2):
+                half_row(t, u)
+                scatter(1, t, h_rows[t][:, BANK * u : BANK * (u + 1)], BANK * u, BANK * (u + 1))
+            if u == 0:
+                for t in range(PACK):
+                    fetch(0, t)
+        for c in range(4):
+            for t in range(PACK):
+                regroup(0, t, c)
+        load_page(1, 3)
+        for t in range(PACK):
+            scale_x(0, t)
+        quantize_x(0)
+        score_pass(0)
+        for t in range(2):
+            fetch(1, t)
+            store_page(1, t)
+        for c in range(2):
+            round_planes(0, c, "scalar")
+            planes(0, c)
+        half_row(2, 0)
+        half_row(2, 1)
+        scatter(1, 2, h_rows[2][:], 0, S)
+        fetch(1, 2)
+        store_page(1, 2)
+        for c in range(2, 4):
+            round_planes(0, c, "scalar")
+            planes(0, c)
+        store_scales(0)
+        half_row(3, 0)
+        half_row(3, 1)
+        scatter(1, 3, h_rows[3][:], 0, S)
+        for c in (2, 3, 0, 1):
+            for t in range(3):
+                regroup(1, t, c)
+        for t in range(3):
+            scale_x(1, t)
+        round_three(2)
+        round_three(3)
+        fetch(1, 3)
+        regroup(1, 3, 1)
+        store_page(1, 3)
+        round_last(2)
+        scale_x(1, 3)
+        round_last(3)
+        regroup(1, 3, 0, by_vector=True)
+        round_planes(1, 0, "vector")
+        planes(1, 2)
+        quantize_x(1)
+        score_pass(1)
+        planes(1, 0)
+        round_planes(1, 1, "vector")
+        planes(1, 3)
+        for n in range(3):
+            y = ring.tile([P, M], F32, name=f"y{n}", tag="h_row", bufs=3)
+            nc.scalar.activation(out=y[:], in_=scores[n][:], func=ACT.Square)
+            nc.sync.dma_start(out=out_0[P * n : P * (n + 1), :], in_=y[:])
+        planes(1, 1)
+        store_scales(1)

@@ -35,7 +35,7 @@ def tile_list_linen_soil_slots_kernel(
         psum = ctx.enter_context(tc.psum_pool(name="psum", bufs=1))
 
         def wide(shape, dtype, name):
-            return ring.tile(shape, dtype, name=name, tag="wide", bufs=4, align_bytes=64)
+            return ring.tile(shape, dtype, name=name, tag="wide", bufs=2, align_bytes=64)
 
         def half(shape, name):
             return ring.tile(shape, BF16, name=name, tag="half", bufs=2, align_bytes=64)
@@ -44,18 +44,18 @@ def tile_list_linen_soil_slots_kernel(
             return ring.tile(shape, dtype, name=name, tag="late", bufs=4, align_bytes=64)
 
         def interleave(engine, dst, src):
-            d = dst.rearrange("p (c i) t -> p c t i", i=4)
-            s = src.rearrange("p t (c i) -> p c t i", i=4)
+            d = dst.rearrange("p (c i) t -> p c t i", i=2)
+            s = src.rearrange("p t (c i) -> p c t i", i=2)
             if engine == "scalar":
                 nc.scalar.copy(out=d, in_=s)
             else:
                 nc.vector.tensor_copy(out=d, in_=s)
 
         def scale_rows(queue, plane, scales):
-            for q in range(4):
+            for r in range(4):
                 queue.dma_start(
-                    out=plane[32 * q : 32 * q + 4, :].bitcast(I32).rearrange("p (a c) -> p a c", a=2),
-                    in_=scales[:, 4 * q : 4 * q + 4, :].rearrange("a r c -> r a c").bitcast(I32),
+                    out=plane[r:P:32, :].bitcast(I32).rearrange("p (a c) -> p a c", a=2),
+                    in_=scales[:, r:16:4, :].rearrange("a q c -> q a c").bitcast(I32),
                 )
 
         list1 = keep.tile([P, S // 16], U16, name="list1")
@@ -72,17 +72,21 @@ def tile_list_linen_soil_slots_kernel(
         svs = keep.tile([P, 2, PACK], F32, name="svs")
         nc.gpsimd.dma_start(out=gains[:], in_=gain.rearrange("(g p t) -> p g t", g=2, t=PACK))
 
+        w1_tiles = {}
+
         def load_w1(g, a):
-            raw = wide([P, PACK, BANK], F32, f"w1raw{g}{a}")
+            if a == 0:
+                w1_tiles[g] = wide([P, 2 * PACK * BANK], F32, f"w1raw{g}")
+            raw = w1_tiles[g][:, PACK * BANK * a : PACK * BANK * (a + 1)].rearrange("p (i c) -> p i c", i=PACK)
             nc.sync.dma_start(
-                out=raw[:],
+                out=raw,
                 in_=w1[PASS * a : PASS * (a + 1), PASS * g : PASS * (g + 1)].rearrange("(p i) c -> p i c", i=PACK),
             )
             return raw
 
         def load_tab(a):
-            words = wide([P, T], U32, f"tab{a}")
-            nc.sync.dma_start(out=words[:].bitcast(I32), in_=tab_words[a].rearrange("p t i -> p (t i)").bitcast(I32))
+            words = tab_tile[:, T * a : T * (a + 1)]
+            nc.sync.dma_start(out=words.bitcast(I32), in_=tab_words[a].rearrange("p t i -> p (t i)").bitcast(I32))
             return words
 
         w2_codes = [keep.tile([P, 2, 2 * PASS], U8, name="w2_codes0", align_bytes=64), late([P, 2, 2 * PASS], U8, "w2_codes1")]
@@ -114,25 +118,27 @@ def tile_list_linen_soil_slots_kernel(
         scale_rows(nc.sync, tab_plane, tab_scales)
         nc.sync.dma_start(list1[:], offs)
         w1_raw[0, 1] = load_w1(0, 1)
-        tabs = [load_tab(0)]
+        tab_tile = wide([P, 2 * T], U32, "tab")
+        tabs = [load_tab(0), load_tab(1)]
         load_w2(0)
-        tabs.append(load_tab(1))
         nc.sync.dma_start(list2[:], offs2)
         load_weights(0, QUARTER)
         for t in range(PACK):
             load_page(0, t)
         load_weights(QUARTER, 2 * QUARTER)
+        load_weights(2 * QUARTER, 3 * QUARTER)
         w1_raw[1, 0] = load_w1(1, 0)
         w1_raw[1, 1] = load_w1(1, 1)
-        load_weights(2 * QUARTER, S)
+        w3_raw = []
+        w3_tile = wide([P, 2 * PACK * N], F32, "w3raw")
+        for g in range(2):
+            raw = w3_tile[:, PACK * N * g : PACK * N * (g + 1)].rearrange("p (i n) -> p i n", i=PACK)
+            nc.sync.dma_start(out=raw, in_=w3[PASS * g : PASS * (g + 1), :].rearrange("(p i) n -> p i n", i=PACK))
+            w3_raw.append(raw)
+        load_weights(3 * QUARTER, S)
         load_w2(1)
         nc.sync.dma_start(list3[:], offs3)
         nc.sync.dma_start(out=svs[:], in_=sv.rearrange("(g p t) -> p g t", g=2, t=PACK))
-        w3_raw = []
-        for g in range(2):
-            raw = wide([P, PACK, N], F32, f"w3raw{g}")
-            nc.sync.dma_start(out=raw[:], in_=w3[PASS * g : PASS * (g + 1), :].rearrange("(p i) n -> p i n", i=PACK))
-            w3_raw.append(raw)
         for t in range(3):
             load_page(1, t)
 
@@ -149,12 +155,12 @@ def tile_list_linen_soil_slots_kernel(
                 grouped = half([P, BANK, PACK], f"w1bf{g}{a}")
             else:
                 grouped = unit_tile([P, BANK, PACK], BF16, a, 2, f"w1bf{g}{a}")
-            interleave("scalar", grouped[:], w1_raw[g, a][:])
+            interleave("scalar", grouped[:], w1_raw[g, a])
             cols = slice((2 * g + a) * BANK, (2 * g + a + 1) * BANK)
             quantize(w1_codes[g][:, a * BANK : (a + 1) * BANK], w1_plane[:, cols], grouped[:].rearrange("p c t -> p (c t)"))
 
         def gather_words(a, j0, j1):
-            nc.vector.tensor_copy(v_codes[a][:, j0:j1], tabs[a][:].indirect(list1[:, j0 // 16 : j1 // 16]))
+            nc.vector.tensor_copy(v_codes[a][:, j0:j1], tabs[a].indirect(list1[:, j0 // 16 : j1 // 16]))
 
         def gather_scales(a, j0, j1):
             window = tab_plane[:, a * T : (a + 1) * T]
@@ -197,13 +203,18 @@ def tile_list_linen_soil_slots_kernel(
                     rhs=w2_codes[g][:, a, :].bitcast(FP4X4),
                     rhs_scale=w2_plane[:, a * H + PASS * g : a * H + PASS * (g + 1)], start=(a == 0), stop=(a == 1),
                 )
-            nc.scalar.activation(out=neg_b, in_=acc_b[:].rearrange("j (p t) -> j t p", t=PACK), func=ACT.Abs)
-            nc.scalar.activation(out=mag_a, in_=acc_a[:].rearrange("j (p t) -> j t p", t=PACK), func=ACT.Abs)
-            nc.scalar.activation(out=neg_b, in_=neg_b, func=ACT.Copy, scale=-1.0)
+            for mag, acc in ((neg_b, acc_b), (mag_a, acc_a)):
+                nc.scalar.activation(
+                    out=mag.rearrange("j t p -> j p t"), in_=acc[:].rearrange("j (p t) -> j p t", t=PACK), func=ACT.Abs
+                )
+            if g == 0 and jb < 2:
+                nc.vector.tensor_scalar_mul(out=neg_b, in0=neg_b, scalar1=-1.0)
+            else:
+                nc.scalar.activation(out=neg_b, in_=neg_b, func=ACT.Copy, scale=-1.0)
 
         def turn(bank, t, jb):
-            nc.tensor.matmul(out=bank, lhsT=mags[0, jb // 2][:, jb % 2, t, :], rhs=ident[:], is_transpose=True, start=True, stop=False)
-            nc.tensor.matmul(out=bank, lhsT=mags[1, jb // 2][:, jb % 2, t, :], rhs=ident[:], is_transpose=True, start=False, stop=True)
+            nc.tensor.matmul(out=bank, lhsT=mags[1, jb // 2][:, jb % 2, t, :], rhs=ident[:], is_transpose=True, start=True, stop=False)
+            nc.tensor.matmul(out=bank, lhsT=mags[0, jb // 2][:, jb % 2, t, :], rhs=ident[:], is_transpose=True, start=False, stop=True)
 
         def scatter(g, t, h, j0, j1):
             nc.vector.tensor_tensor(
@@ -215,21 +226,25 @@ def tile_list_linen_soil_slots_kernel(
                 bank = bank_tile([P, QUARTER], 4 + t, "turned")
                 for b in range(2):
                     turn(bank[:, P * b : P * (b + 1)], t, 2 * q + b)
-                h = ring.tile([P, QUARTER], F32, name="h_quarter", tag="h_quarter", bufs=8)
-                nc.scalar.activation(out=h[:], in_=bank[:], func=ACT.Copy, scale=gains[:, 0, t : t + 1])
-                scatter(0, t, h[:], QUARTER * q, QUARTER * (q + 1))
+                if q < 3:
+                    h = ring.tile([P, QUARTER], F32, name="h_quarter", tag="h_quarter", bufs=8)[:]
+                else:
+                    h = w1_tiles[1][:, PACK * BANK + QUARTER * t : PACK * BANK + QUARTER * (t + 1)]
+                nc.scalar.activation(out=h, in_=bank[:], func=ACT.Copy, scale=gains[:, 0, t : t + 1])
+                scatter(0, t, h, QUARTER * q, QUARTER * (q + 1))
 
         h_rows = {}
 
-        def half_row(t, u):
+        def half_row(t, u, h=None):
             if u == 0:
                 h_rows[t] = ring.tile([P, S], F32, name=f"h_row{t}", tag="h_row", bufs=3)
+            if h is None:
+                h = h_rows[t][:, BANK * u : BANK * (u + 1)]
             bank = bank_tile([P, BANK], (2 * u + t) % 4 if t < 2 else 2 * (t - 2) + u, "turned")
             for b in range(4):
                 turn(bank[:, P * b : P * (b + 1)], t, 4 * u + b)
-            nc.scalar.activation(
-                out=h_rows[t][:, BANK * u : BANK * (u + 1)], in_=bank[:], func=ACT.Copy, scale=gains[:, 1, t : t + 1]
-            )
+            nc.scalar.activation(out=h, in_=bank[:], func=ACT.Copy, scale=gains[:, 1, t : t + 1])
+            return h
 
         x_codes = [keep.tile([P, M], U32, name=f"x_codes{g}", align_bytes=64) for g in range(2)]
         x_plane = [keep.tile([P, M], U8, name=f"x_plane{g}", align_bytes=64) for g in range(2)]
@@ -258,14 +273,19 @@ def tile_list_linen_soil_slots_kernel(
 
         stages = {}
 
-        def regroup(g, t, c, by_vector=False):
-            if (g, c) not in stages:
-                stages[g, c] = wide([P, PACK, BANK], F32, f"stage{g}{c}")
-            src = pages[g, t][:, BANK * c : BANK * (c + 1)]
-            if by_vector:
-                nc.vector.tensor_copy(out=stages[g, c][:, t, :], in_=src)
-            else:
-                nc.sync.dma_start(out=stages[g, c][:, t, :], in_=src)
+        def staged(g, c):
+            tile = stages[g, c // 2][:].rearrange("p (t m) -> p t m", t=PACK)
+            return tile[:, :, BANK * (c % 2) : BANK * (c % 2 + 1)]
+
+        def regroup(g, t, u):
+            if (g, u) not in stages:
+                stages[g, u] = wide([P, PACK * 2 * BANK], F32, f"stage{g}{u}")
+            nc.sync.dma_start(
+                out=stages[g, u][:, 2 * BANK * t : 2 * BANK * (t + 1)], in_=pages[g, t][:, 2 * BANK * u : 2 * BANK * (u + 1)]
+            )
+
+        def regroup_chunk(t, c):
+            nc.sync.dma_start(out=staged(1, c)[:, t, :], in_=pages[1, t][:, BANK * c : BANK * (c + 1)])
 
         y_planes = [keep.tile([P, T2], U8, name=f"y_plane{g}", align_bytes=64) for g in range(2)]
 
@@ -273,11 +293,11 @@ def tile_list_linen_soil_slots_kernel(
 
         def round_planes(g, c, engine):
             rounded[g, c] = late([P, BANK, PACK], BF16, f"ybf{g}{c}")
-            interleave(engine, rounded[g, c][:], stages[g, c][:])
+            interleave(engine, rounded[g, c][:], staged(g, c))
 
         def round_three(c):
             rounded[1, c] = half([P, BANK, PACK], f"ybf1{c}")
-            interleave("scalar", rounded[1, c][:, :, 0:3], stages[1, c][:, 0:3, :])
+            interleave("scalar", rounded[1, c][:, :, 0:3], staged(1, c)[:, 0:3, :])
 
         def round_last(c):
             nc.scalar.copy(out=rounded[1, c][:, :, 3], in_=pages[1, 3][:, BANK * c : BANK * (c + 1)])
@@ -292,17 +312,15 @@ def tile_list_linen_soil_slots_kernel(
             )
 
         def store_scales(g):
-            for q in range(4):
-                nc.sync.dma_start(
-                    out=out_3[g, 4 * q : 4 * q + 4, :].bitcast(I32), in_=y_planes[g][32 * q : 32 * q + 4, :].bitcast(I32)
-                )
+            for r in range(4):
+                nc.sync.dma_start(out=out_3[g, r:16:4, :].bitcast(I32), in_=y_planes[g][r:P:32, :].bitcast(I32))
 
         w3_codes = keep.tile([P, 2 * N], U32, name="w3_codes", align_bytes=64)
         w3_plane = keep.tile([P, 2 * N], U8, name="w3_plane", align_bytes=64)
 
         def quantize_w3(g):
             grouped = unit_tile([P, N, PACK], BF16, g, 3, f"w3bf{g}")
-            interleave("scalar", grouped[:], w3_raw[g][:])
+            interleave("vector", grouped[:], w3_raw[g])
             for c0, c1 in ((0, 256), (256, N)):
                 quantize(
                     w3_codes[:, N * g + c0 : N * g + c1], w3_plane[:, N * g + c0 : N * g + c1],
@@ -330,22 +348,21 @@ def tile_list_linen_soil_slots_kernel(
             quarter_unit(q)
         quantize_w3(0)
         quantize_w3(1)
+        for u in range(2):
+            for t in range(PACK):
+                regroup(0, t, u)
         for t in range(PACK):
             store_page(0, t)
+        load_page(1, 3)
 
         for u in range(2):
             for jb in range(4 * u, 4 * u + 4):
                 magnitudes(1, jb)
             for t in range(2):
-                half_row(t, u)
-                scatter(1, t, h_rows[t][:, BANK * u : BANK * (u + 1)], BANK * u, BANK * (u + 1))
+                scatter(1, t, half_row(t, u), BANK * u, BANK * (u + 1))
             if u == 0:
                 for t in range(PACK):
                     fetch(0, t)
-        for c in range(4):
-            for t in range(PACK):
-                regroup(0, t, c)
-        load_page(1, 3)
         for t in range(PACK):
             scale_x(0, t)
         quantize_x(0)
@@ -356,42 +373,46 @@ def tile_list_linen_soil_slots_kernel(
         for c in range(2):
             round_planes(0, c, "scalar")
             planes(0, c)
+        regroup(1, 0, 0)
+        regroup(1, 1, 0)
         half_row(2, 0)
         half_row(2, 1)
         scatter(1, 2, h_rows[2][:], 0, S)
         fetch(1, 2)
-        store_page(1, 2)
         for c in range(2, 4):
             round_planes(0, c, "scalar")
+        regroup(1, 0, 1)
+        regroup(1, 1, 1)
+        regroup_chunk(2, 0)
+        regroup(1, 2, 1)
+        regroup_chunk(2, 1)
+        for c in range(2, 4):
             planes(0, c)
+        store_page(1, 2)
         store_scales(0)
-        half_row(3, 0)
-        half_row(3, 1)
-        scatter(1, 3, h_rows[3][:], 0, S)
-        for c in (2, 3, 0, 1):
-            for t in range(3):
-                regroup(1, t, c)
+        scatter(1, 3, half_row(3, 0), 0, BANK)
         for t in range(3):
             scale_x(1, t)
-        round_three(2)
-        round_three(3)
+        round_three(0)
+        scatter(1, 3, half_row(3, 1, staged(1, 0)[:, 0, :]), BANK, S)
+        round_three(1)
         fetch(1, 3)
-        regroup(1, 3, 1)
+        regroup_chunk(3, 3)
         store_page(1, 3)
-        round_last(2)
+        round_last(0)
         scale_x(1, 3)
-        round_last(3)
-        regroup(1, 3, 0, by_vector=True)
-        round_planes(1, 0, "vector")
-        planes(1, 2)
+        round_last(1)
+        nc.vector.tensor_copy(out=staged(1, 2)[:, 3, :], in_=pages[1, 3][:, 2 * BANK : 3 * BANK])
+        round_planes(1, 2, "vector")
+        planes(1, 0)
         quantize_x(1)
         score_pass(1)
-        planes(1, 0)
-        round_planes(1, 1, "vector")
-        planes(1, 3)
+        planes(1, 2)
+        round_planes(1, 3, "vector")
+        planes(1, 1)
         for n in range(3):
             y = ring.tile([P, M], F32, name=f"y{n}", tag="h_row", bufs=3)
             nc.scalar.activation(out=y[:], in_=scores[n][:], func=ACT.Square)
             nc.sync.dma_start(out=out_0[P * n : P * (n + 1), :], in_=y[:])
-        planes(1, 1)
+        planes(1, 3)
         store_scales(1)

@@ -22,6 +22,7 @@ PACK = 4
 PASS = P * PACK
 BANK = 512
 QUARTER = 256
+ALIGN = 256
 
 
 def tile_list_linen_soil_slots_kernel(
@@ -34,14 +35,20 @@ def tile_list_linen_soil_slots_kernel(
         ring = ctx.enter_context(tc.tile_pool(name="ring", bufs=1))
         psum = ctx.enter_context(tc.psum_pool(name="psum", bufs=1))
 
-        def wide(shape, dtype, name):
-            return ring.tile(shape, dtype, name=name, tag="wide", bufs=2, align_bytes=64)
+        def wide(shape, dtype, side, name):
+            return ring.tile(shape, dtype, name=name, tag=f"wide{side}", bufs=1, align_bytes=ALIGN)
 
-        def half(shape, name):
-            return ring.tile(shape, BF16, name=name, tag="half", bufs=2, align_bytes=64)
+        def relay(shape, dtype, name):
+            return ring.tile(shape, dtype, name=name, tag="relay", bufs=1, align_bytes=ALIGN)
 
         def late(shape, dtype, name):
-            return ring.tile(shape, dtype, name=name, tag="late", bufs=4, align_bytes=64)
+            return ring.tile(shape, dtype, name=name, tag="late", bufs=4, align_bytes=ALIGN)
+
+        def bank_tile(shape, n, name):
+            return psum.tile(shape, F32, name=name, tag=f"bank{n}", bufs=1)
+
+        def unit_tile(shape, dtype, side, q, name):
+            return ring.tile(shape, dtype, name=name, tag=f"unit{side}{q}", bufs=1, align_bytes=ALIGN)
 
         def interleave(engine, dst, src):
             d = dst.rearrange("p (c i) t -> p c t i", i=2)
@@ -61,13 +68,13 @@ def tile_list_linen_soil_slots_kernel(
         list1 = keep.tile([P, S // 16], U16, name="list1")
         list2 = keep.tile([P, S // 16], U16, name="list2")
         list3 = keep.tile([P, M // 16], U16, name="list3")
-        tab_plane = keep.tile([P, 2 * T], U8, name="tab_plane", align_bytes=64)
-        w2_plane = keep.tile([P, 2 * H], U8, name="w2_plane", align_bytes=64)
+        tab_plane = keep.tile([P, T], U8, name="tab_plane", align_bytes=ALIGN)
+        w2_plane = keep.tile([P, 2 * H], U8, name="w2_plane", align_bytes=ALIGN)
         nc.vector.memset(tab_plane[:].bitcast(I32), 0)
-        nc.gpsimd.memset(w2_plane[:].bitcast(I32), 0)
-        scale_rows(nc.gpsimd, w2_plane, w2_scales)
+        nc.vector.memset(w2_plane[:].bitcast(I32), 0)
         ident = keep.tile([P, P], F32, name="ident")
         make_identity(nc, ident[:])
+        scale_rows(nc.gpsimd, w2_plane, w2_scales)
         gains = keep.tile([P, 2, PACK], F32, name="gains")
         svs = keep.tile([P, 2, PACK], F32, name="svs")
         nc.gpsimd.dma_start(out=gains[:], in_=gain.rearrange("(g p t) -> p g t", g=2, t=PACK))
@@ -76,7 +83,7 @@ def tile_list_linen_soil_slots_kernel(
 
         def load_w1(g, a):
             if a == 0:
-                w1_tiles[g] = wide([P, 2 * PACK * BANK], F32, f"w1raw{g}")
+                w1_tiles[g] = wide([P, 2 * PACK * BANK], F32, 1, f"w1raw{g}")
             raw = w1_tiles[g][:, PACK * BANK * a : PACK * BANK * (a + 1)].rearrange("p (i c) -> p i c", i=PACK)
             nc.sync.dma_start(
                 out=raw,
@@ -89,7 +96,8 @@ def tile_list_linen_soil_slots_kernel(
             nc.sync.dma_start(out=words.bitcast(I32), in_=tab_words[a].rearrange("p t i -> p (t i)").bitcast(I32))
             return words
 
-        w2_codes = [keep.tile([P, 2, 2 * PASS], U8, name="w2_codes0", align_bytes=64), late([P, 2, 2 * PASS], U8, "w2_codes1")]
+        v_codes = [late([P, S], U32, f"v_codes{a}") for a in range(2)]
+        w2_codes = [keep.tile([P, 2, 2 * PASS], U8, name="w2_codes0", align_bytes=ALIGN), late([P, 2, 2 * PASS], U8, "w2_codes1")]
 
         def load_w2(g):
             nc.sync.dma_start(
@@ -99,109 +107,122 @@ def tile_list_linen_soil_slots_kernel(
 
         weights = keep.tile([P, PACK, S], F32, name="weights")
 
-        def load_weights(j0, j1):
-            for q in (0, 2, 1, 3):
-                nc.sync.dma_start(
-                    out=weights[32 * q : 32 * (q + 1), :, j0:j1],
-                    in_=wgs[:, j0:j1].rearrange("(p t) j -> p t j", t=PACK),
-                )
-
         pages = {}
         page_in = page0.rearrange("(g p t) m -> g t p m", g=2, t=PACK)
         page_out = out_1.rearrange("(g p t) m -> g t p m", g=2, t=PACK)
 
         def load_page(g, t):
-            pages[g, t] = ring.tile([P, T2], F32, name=f"page{g}{t}", tag="page", bufs=7)
+            pages[g, t] = ring.tile([P, T2], F32, name=f"page{g}{t}", tag="page", bufs=8, align_bytes=ALIGN)
             nc.sync.dma_start(out=pages[g, t][:], in_=page_in[g, t])
 
+        wgs_rows = unit_tile([P, S], F32, 0, 1, "wgs_rows")
+        nc.sync.dma_start(out=wgs_rows[:], in_=wgs)
         w1_raw = {(0, 0): load_w1(0, 0)}
-        scale_rows(nc.sync, tab_plane, tab_scales)
+        for q in range(4):
+            nc.sync.dma_start(
+                out=tab_plane[32 * q : 32 * q + 8, :].bitcast(I32), in_=tab_scales[:, 4 * q : 4 * q + 4, :].bitcast(I32)
+            )
         nc.sync.dma_start(list1[:], offs)
         w1_raw[0, 1] = load_w1(0, 1)
-        tab_tile = wide([P, 2 * T], U32, "tab")
-        tabs = [load_tab(0), load_tab(1)]
+        tab_tile = wide([P, 2 * T], U32, 0, "tab")
         load_w2(0)
+        tabs = [load_tab(0)]
+        v_plane = keep.tile([P, S], U8, name="v_plane", align_bytes=ALIGN)
+        v_plane_moved = keep.tile([P, S], U8, name="v_plane_moved", align_bytes=ALIGN)
+        nc.vector.memset(v_plane_moved[:].bitcast(I32), 0)
+        nc.vector.tensor_copy(v_plane[:], tab_plane[:].indirect(list1[:]))
+        for r in range(4):
+            nc.sync.dma_start(out=v_plane_moved[r:P:32, :].bitcast(I32), in_=v_plane[4 + r : P : 32, :].bitcast(I32))
+        tabs.append(load_tab(1))
         nc.sync.dma_start(list2[:], offs2)
-        load_weights(0, QUARTER)
         for t in range(PACK):
             load_page(0, t)
-        load_weights(QUARTER, 2 * QUARTER)
-        load_weights(2 * QUARTER, 3 * QUARTER)
         w1_raw[1, 0] = load_w1(1, 0)
         w1_raw[1, 1] = load_w1(1, 1)
         w3_raw = []
-        w3_tile = wide([P, 2 * PACK * N], F32, "w3raw")
+        w3_tile = wide([P, 2 * PACK * N], F32, 0, "w3raw")
         for g in range(2):
             raw = w3_tile[:, PACK * N * g : PACK * N * (g + 1)].rearrange("p (i n) -> p i n", i=PACK)
             nc.sync.dma_start(out=raw, in_=w3[PASS * g : PASS * (g + 1), :].rearrange("(p i) n -> p i n", i=PACK))
             w3_raw.append(raw)
-        load_weights(3 * QUARTER, S)
         load_w2(1)
         nc.sync.dma_start(list3[:], offs3)
         nc.sync.dma_start(out=svs[:], in_=sv.rearrange("(g p t) -> p g t", g=2, t=PACK))
-        for t in range(3):
+        for t in range(PACK):
             load_page(1, t)
 
-        v_codes = [late([P, S], U32, f"v_codes{a}") for a in range(2)]
-        v_plane = [keep.tile([P, S], U8, name=f"v_plane{a}", align_bytes=64) for a in range(2)]
-        w1_codes = [keep.tile([P, 2 * BANK], U32, name="w1_codes0", align_bytes=64), late([P, 2 * BANK], U32, "w1_codes1")]
-        w1_plane = keep.tile([P, 4 * BANK], U8, name="w1_plane", align_bytes=64)
+        repeated = {}
+        for u in (1, 0):
+            bank = bank_tile([P, 4, P], u, "wgs_turned")
+            for b in range(4):
+                jb = 4 * u + b
+                nc.tensor.transpose(bank[:, b, :], wgs_rows[:, P * jb : P * (jb + 1)], ident[:])
+            for e in range(2):
+                repeated[u, e] = unit_tile([P, 2, PACK, P], F32, e, 2 + u, f"wgs_repeated{u}{e}")
+                nc.scalar.copy(
+                    out=repeated[u, e][:].rearrange("j b t (k v) -> j b k v t", k=4),
+                    in_=bank[:, 2 * e : 2 * e + 2, :].rearrange("j b (k v t) -> j b k v t", k=1, t=PACK).to_broadcast([P, 2, 4, 32, PACK]),
+                )
+
+        def deal_weights(u):
+            for t in range(PACK):
+                bank = bank_tile([P, BANK], 4 * (1 - u) + t, "wgs_dealt")
+                for b in range(4):
+                    nc.tensor.transpose(bank[:, P * b : P * (b + 1)], repeated[u, b // 2][:, b % 2, t, :], ident[:])
+                nc.scalar.copy(out=weights[:, t, BANK * u : BANK * (u + 1)], in_=bank[:])
+
+        w1_codes = [keep.tile([P, 2 * BANK], U32, name="w1_codes0", align_bytes=ALIGN), late([P, 2 * BANK], U32, "w1_codes1")]
+        w1_plane = keep.tile([P, 4 * BANK], U8, name="w1_plane", align_bytes=ALIGN)
 
         def quantize(codes, plane, grouped):
             nc.vector.quantize_mx(out=codes.bitcast(FP8X4), scales=plane, in_=grouped)
 
-        def quantize_w1(g, a):
-            if g == 0:
-                grouped = half([P, BANK, PACK], f"w1bf{g}{a}")
-            else:
-                grouped = unit_tile([P, BANK, PACK], BF16, a, 2, f"w1bf{g}{a}")
-            interleave("scalar", grouped[:], w1_raw[g, a])
-            cols = slice((2 * g + a) * BANK, (2 * g + a + 1) * BANK)
-            quantize(w1_codes[g][:, a * BANK : (a + 1) * BANK], w1_plane[:, cols], grouped[:].rearrange("p c t -> p (c t)"))
+        def quantize_w1(g):
+            grouped = relay([P, 2 * BANK * PACK], BF16, f"w1bf{g}")
+            for a in range(2):
+                part = grouped[:, a * BANK * PACK : (a + 1) * BANK * PACK]
+                interleave("vector" if g == 0 else "scalar", part.rearrange("p (c t) -> p c t", t=PACK), w1_raw[g, a])
+                if g == 0:
+                    quantize(w1_codes[0][:, a * BANK : (a + 1) * BANK], w1_plane[:, a * BANK : (a + 1) * BANK], part)
+            if g == 1:
+                quantize(w1_codes[1][:], w1_plane[:, 2 * BANK : 4 * BANK], grouped[:])
 
         def gather_words(a, j0, j1):
             nc.vector.tensor_copy(v_codes[a][:, j0:j1], tabs[a].indirect(list1[:, j0 // 16 : j1 // 16]))
 
-        def gather_scales(a, j0, j1):
-            window = tab_plane[:, a * T : (a + 1) * T]
-            nc.vector.tensor_copy(v_plane[a][:, j0:j1], window.indirect(list1[:, j0 // 16 : j1 // 16]))
-
-        for a in range(2):
-            quantize_w1(0, a)
-        for a in range(2):
-            gather_scales(a, 0, S)
+        quantize_w1(0)
+        deal_weights(1)
+        deal_weights(0)
         for j0, j1 in ((0, QUARTER), (QUARTER, S)):
             for a in range(2):
                 gather_words(a, j0, j1)
 
         mags = {}
 
-        def bank_tile(shape, n, name):
-            return psum.tile(shape, F32, name=name, tag=f"bank{n}", bufs=1)
-
-        def unit_tile(shape, dtype, side, q, name):
-            return ring.tile(shape, dtype, name=name, tag=f"unit{side}{q}", bufs=1, align_bytes=64)
-
         def magnitudes(g, jb):
-            if jb % 2 == 0:
+            if (g, jb) == (0, 2):
+                both = relay([P, 2, 2, PACK, P], F32, "mag_unit1")
+                mags[0, 1], mags[1, 1] = both[:, 0], both[:, 1]
+            elif jb % 2 == 0:
                 for side in range(2):
                     mags[side, jb // 2] = unit_tile([P, 2, PACK, P], F32, side, jb // 2, f"mag{g}{side}{jb // 2}")
             mag_a = mags[0, jb // 2][:, jb % 2]
             neg_b = mags[1, jb // 2][:, jb % 2]
             js = slice(P * jb, P * (jb + 1))
-            acc_a = bank_tile([P, BANK], 4 * g + 2 * (jb % 2), "acc_a")
-            acc_b = bank_tile([P, BANK], 4 * g + 2 * (jb % 2) + 1, "acc_b")
+            first = 4 if g == 0 and jb >= 2 else 0
+            acc_a = bank_tile([P, BANK], first + 2 * (jb % 2), "acc_a")
+            acc_b = bank_tile([P, BANK], first + 2 * (jb % 2) + 1, "acc_b")
+            for a in range(2):
+                nc.tensor.matmul_mx(
+                    out=acc_b[:], lhsT=v_codes[a][:, js].bitcast(FP8X4), lhsT_scale=(v_plane, v_plane_moved)[a][:, js],
+                    rhs=w2_codes[g][:, a, :].bitcast(FP4X4),
+                    rhs_scale=w2_plane[:, a * H + PASS * g : a * H + PASS * (g + 1)], start=(a == 0), stop=(a == 1),
+                )
             for a in range(2):
                 cols = slice((2 * g + a) * BANK, (2 * g + a + 1) * BANK)
                 nc.tensor.matmul_mx(
-                    out=acc_a[:], lhsT=v_codes[a][:, js].bitcast(FP8X4), lhsT_scale=v_plane[a][:, js],
+                    out=acc_a[:], lhsT=v_codes[a][:, js].bitcast(FP8X4), lhsT_scale=v_plane[4 * a : P, js],
                     rhs=w1_codes[g][:, a * BANK : (a + 1) * BANK].bitcast(FP8X4), rhs_scale=w1_plane[:, cols], start=(a == 0), stop=(a == 1),
-                )
-            for a in range(2):
-                nc.tensor.matmul_mx(
-                    out=acc_b[:], lhsT=v_codes[a][:, js].bitcast(FP8X4), lhsT_scale=v_plane[a][:, js],
-                    rhs=w2_codes[g][:, a, :].bitcast(FP4X4),
-                    rhs_scale=w2_plane[:, a * H + PASS * g : a * H + PASS * (g + 1)], start=(a == 0), stop=(a == 1),
                 )
             for mag, acc in ((neg_b, acc_b), (mag_a, acc_a)):
                 nc.scalar.activation(
@@ -222,51 +243,61 @@ def tile_list_linen_soil_slots_kernel(
             )
 
         def quarter_unit(q):
-            for t in range(PACK):
-                bank = bank_tile([P, QUARTER], 4 + t, "turned")
+            for t in range(PACK if q < 2 else PACK - 1):
+                bank = bank_tile([P, QUARTER], (4 if q == 0 else 0) + t, "turned")
                 for b in range(2):
                     turn(bank[:, P * b : P * (b + 1)], t, 2 * q + b)
-                if q < 3:
-                    h = ring.tile([P, QUARTER], F32, name="h_quarter", tag="h_quarter", bufs=8)[:]
-                else:
-                    h = w1_tiles[1][:, PACK * BANK + QUARTER * t : PACK * BANK + QUARTER * (t + 1)]
-                nc.scalar.activation(out=h, in_=bank[:], func=ACT.Copy, scale=gains[:, 0, t : t + 1])
-                scatter(0, t, h, QUARTER * q, QUARTER * (q + 1))
+                h = ring.tile([P, QUARTER], F32, name="h_quarter", tag="h_quarter", bufs=7)
+                nc.scalar.activation(out=h[:], in_=bank[:], func=ACT.Copy, scale=gains[:, 0, t : t + 1])
+                scatter(0, t, h[:], QUARTER * q, QUARTER * (q + 1))
+
+        def turn_last_tile():
+            bank = bank_tile([P, BANK], 3, "turned")
+            for b in range(4):
+                turn(bank[:, P * b : P * (b + 1)], 3, 4 + b)
+            return bank
+
+        def scatter_last_tile(bank):
+            h = w1_tiles[1][:, PACK * BANK : PACK * BANK + BANK]
+            nc.scalar.activation(out=h, in_=bank[:], func=ACT.Copy, scale=gains[:, 0, 3:4])
+            scatter(0, 3, h, BANK, S)
 
         h_rows = {}
+        next_bank = [0, 1, 2, 3, 0, 1, 2, 3]
 
         def half_row(t, u, h=None):
             if u == 0:
-                h_rows[t] = ring.tile([P, S], F32, name=f"h_row{t}", tag="h_row", bufs=3)
+                h_rows[t] = ring.tile([P, S], F32, name=f"h_row{t}", tag="h_row", bufs=3, align_bytes=ALIGN)
             if h is None:
                 h = h_rows[t][:, BANK * u : BANK * (u + 1)]
-            bank = bank_tile([P, BANK], (2 * u + t) % 4 if t < 2 else 2 * (t - 2) + u, "turned")
+            bank = bank_tile([P, BANK], 4 + next_bank.pop(0), "turned")
             for b in range(4):
                 turn(bank[:, P * b : P * (b + 1)], t, 4 * u + b)
             nc.scalar.activation(out=h, in_=bank[:], func=ACT.Copy, scale=gains[:, 1, t : t + 1])
             return h
 
-        x_codes = [keep.tile([P, M], U32, name=f"x_codes{g}", align_bytes=64) for g in range(2)]
-        x_plane = [keep.tile([P, M], U8, name=f"x_plane{g}", align_bytes=64) for g in range(2)]
+        x_codes = [keep.tile([P, M], U32, name=f"x_codes{g}", align_bytes=ALIGN) for g in range(2)]
+        x_plane = [keep.tile([P, M], U8, name=f"x_plane{g}", align_bytes=ALIGN) for g in range(2)]
         x_tiles = {}
+        x_rows = {}
         picked = {}
 
-        def fetch(g, t):
-            picked[g, t] = ring.tile([P, M], F32, name="picked", tag="picked", bufs=4)
-            nc.vector.tensor_copy(picked[g, t][:], pages[g, t][:].indirect(list3[:]))
+        def fetch(g, t, dst=None):
+            picked[g, t] = ring.tile([P, M], F32, name="picked", tag="picked", bufs=3)[:] if dst is None else dst
+            nc.vector.tensor_copy(picked[g, t], pages[g, t][:].indirect(list3[:]))
 
         def scale_x(g, t):
             if t == 0:
-                x_tiles[g] = late([P, PACK, M], BF16, "x_rows") if g == 0 else late([P, M, PACK], BF16, "xbf1")
-            dst = x_tiles[g][:, t, :] if g == 0 else x_tiles[g][:, :, t]
-            nc.scalar.activation(out=dst, in_=picked[g, t][:], func=ACT.Copy, scale=svs[:, g, t : t + 1])
+                x_rows[g] = late([P, PACK, M], BF16, f"x_rows{g}")
+            dst = x_tiles[1][:, :, 3] if (g, t) == (1, 3) else x_rows[g][:, t, :]
+            nc.scalar.activation(out=dst, in_=picked[g, t], func=ACT.Copy, scale=svs[:, g, t : t + 1])
+
+        def weave_x(g, rows):
+            x_tiles[g] = (relay, late)[g]([P, M, PACK], BF16, f"xbf{g}")
+            interleave("scalar", x_tiles[g][:, :, 0:rows], x_rows[g][:, 0:rows, :])
 
         def quantize_x(g):
-            grouped = x_tiles[g]
-            if g == 0:
-                grouped = late([P, M, PACK], BF16, "xbf0")
-                interleave("scalar", grouped[:], x_tiles[g][:])
-            quantize(x_codes[g][:], x_plane[g][:], grouped[:].rearrange("p c t -> p (c t)"))
+            quantize(x_codes[g][:], x_plane[g][:], x_tiles[g][:].rearrange("p c t -> p (c t)"))
 
         def store_page(g, t):
             nc.sync.dma_start(out=page_out[g, t], in_=pages[g, t][:])
@@ -279,15 +310,12 @@ def tile_list_linen_soil_slots_kernel(
 
         def regroup(g, t, u):
             if (g, u) not in stages:
-                stages[g, u] = wide([P, PACK * 2 * BANK], F32, f"stage{g}{u}")
+                stages[g, u] = wide([P, PACK * 2 * BANK], F32, u, f"stage{g}{u}")
             nc.sync.dma_start(
                 out=stages[g, u][:, 2 * BANK * t : 2 * BANK * (t + 1)], in_=pages[g, t][:, 2 * BANK * u : 2 * BANK * (u + 1)]
             )
 
-        def regroup_chunk(t, c):
-            nc.sync.dma_start(out=staged(1, c)[:, t, :], in_=pages[1, t][:, BANK * c : BANK * (c + 1)])
-
-        y_planes = [keep.tile([P, T2], U8, name=f"y_plane{g}", align_bytes=64) for g in range(2)]
+        y_planes = [keep.tile([P, T2], U8, name=f"y_plane{g}", align_bytes=ALIGN) for g in range(2)]
 
         rounded = {}
 
@@ -296,7 +324,9 @@ def tile_list_linen_soil_slots_kernel(
             interleave(engine, rounded[g, c][:], staged(g, c))
 
         def round_three(c):
-            rounded[1, c] = half([P, BANK, PACK], f"ybf1{c}")
+            if c == 0:
+                rounded["pair"] = relay([P, 2 * BANK * PACK], BF16, "ybf1pair")
+            rounded[1, c] = rounded["pair"][:, BANK * PACK * c : BANK * PACK * (c + 1)].rearrange("p (c t) -> p c t", t=PACK)
             interleave("scalar", rounded[1, c][:, :, 0:3], staged(1, c)[:, 0:3, :])
 
         def round_last(c):
@@ -305,7 +335,7 @@ def tile_list_linen_soil_slots_kernel(
         def planes(g, c):
             cols = slice(BANK * c, BANK * (c + 1))
             grouped = rounded[g, c]
-            codes = ring.tile([P, BANK], U32, name="y_codes", tag="y_codes", bufs=4, align_bytes=64)
+            codes = ring.tile([P, BANK], U32, name="y_codes", tag="y_codes", bufs=6, align_bytes=ALIGN)
             quantize(codes[:], y_planes[g][:, cols], grouped[:].rearrange("p c t -> p (c t)"))
             nc.sync.dma_start(
                 out=out_2[g, :, cols, :].rearrange("p m t -> p (m t)").bitcast(I32), in_=codes[:].bitcast(I32)
@@ -315,12 +345,15 @@ def tile_list_linen_soil_slots_kernel(
             for r in range(4):
                 nc.sync.dma_start(out=out_3[g, r:16:4, :].bitcast(I32), in_=y_planes[g][r:P:32, :].bitcast(I32))
 
-        w3_codes = keep.tile([P, 2 * N], U32, name="w3_codes", align_bytes=64)
-        w3_plane = keep.tile([P, 2 * N], U8, name="w3_plane", align_bytes=64)
+        w3_codes = keep.tile([P, 2 * N], U32, name="w3_codes", align_bytes=ALIGN)
+        w3_plane = keep.tile([P, 2 * N], U8, name="w3_plane", align_bytes=ALIGN)
 
         def quantize_w3(g):
-            grouped = unit_tile([P, N, PACK], BF16, g, 3, f"w3bf{g}")
-            interleave("vector", grouped[:], w3_raw[g])
+            if g == 0:
+                grouped = unit_tile([P, N, PACK], BF16, 0, 3, "w3bf0")
+            else:
+                grouped = relay([P, N, PACK], BF16, "w3bf1")
+            interleave(("scalar", "vector")[g], grouped[:], w3_raw[g])
             for c0, c1 in ((0, 256), (256, N)):
                 quantize(
                     w3_codes[:, N * g + c0 : N * g + c1], w3_plane[:, N * g + c0 : N * g + c1],
@@ -332,7 +365,7 @@ def tile_list_linen_soil_slots_kernel(
         def score_pass(g):
             for n in range(3):
                 if g == 0:
-                    scores[n] = bank_tile([P, M], 4 + n, f"score{n}")
+                    scores[n] = bank_tile([P, M], n, f"score{n}")
                 cols = slice(N * g + P * n, N * g + P * (n + 1))
                 nc.tensor.matmul_mx(
                     out=scores[n][:], lhsT=w3_codes[:, cols].bitcast(FP8X4), lhsT_scale=w3_plane[:, cols],
@@ -340,78 +373,78 @@ def tile_list_linen_soil_slots_kernel(
                 )
 
         for q in range(4):
-            if q == 3:
-                quantize_w1(1, 0)
-                quantize_w1(1, 1)
             magnitudes(0, 2 * q)
             magnitudes(0, 2 * q + 1)
             quarter_unit(q)
+        last_banks = turn_last_tile()
+        for t in range(3):
+            store_page(0, t)
+        quantize_w1(1)
+        scatter_last_tile(last_banks)
         quantize_w3(0)
         quantize_w3(1)
+        picked_rows = relay([P, PACK * M], F32, "picked_rows")
+        for t in range(PACK):
+            fetch(0, t, picked_rows[:, M * t : M * (t + 1)])
         for u in range(2):
             for t in range(PACK):
                 regroup(0, t, u)
-        for t in range(PACK):
-            store_page(0, t)
-        load_page(1, 3)
+        store_page(0, 3)
 
         for u in range(2):
             for jb in range(4 * u, 4 * u + 4):
                 magnitudes(1, jb)
-            for t in range(2):
+            for t in range(3 - u):
                 scatter(1, t, half_row(t, u), BANK * u, BANK * (u + 1))
-            if u == 0:
-                for t in range(PACK):
-                    fetch(0, t)
         for t in range(PACK):
             scale_x(0, t)
-        quantize_x(0)
-        score_pass(0)
-        for t in range(2):
-            fetch(1, t)
-            store_page(1, t)
-        for c in range(2):
-            round_planes(0, c, "scalar")
-            planes(0, c)
+        fetch(1, 0)
+        fetch(1, 1)
+        store_page(1, 0)
+        scatter(1, 2, half_row(2, 1), BANK, S)
+        fetch(1, 2)
+        round_planes(0, 0, "scalar")
+        round_planes(0, 1, "scalar")
+        weave_x(0, PACK)
+        round_planes(0, 2, "scalar")
+        round_planes(0, 3, "scalar")
         regroup(1, 0, 0)
         regroup(1, 1, 0)
-        half_row(2, 0)
-        half_row(2, 1)
-        scatter(1, 2, h_rows[2][:], 0, S)
-        fetch(1, 2)
-        for c in range(2, 4):
-            round_planes(0, c, "scalar")
-        regroup(1, 0, 1)
-        regroup(1, 1, 1)
-        regroup_chunk(2, 0)
-        regroup(1, 2, 1)
-        regroup_chunk(2, 1)
-        for c in range(2, 4):
-            planes(0, c)
+        store_page(1, 1)
+        regroup(1, 2, 0)
         store_page(1, 2)
+        for t in range(3):
+            regroup(1, t, 1)
+        planes(0, 0)
+        planes(0, 1)
+        quantize_x(0)
+        score_pass(0)
+        planes(0, 2)
+        planes(0, 3)
         store_scales(0)
-        scatter(1, 3, half_row(3, 0), 0, BANK)
+        half_row(3, 0)
+        half_row(3, 1)
+        scatter(1, 3, h_rows[3][:], 0, S)
         for t in range(3):
             scale_x(1, t)
         round_three(0)
-        scatter(1, 3, half_row(3, 1, staged(1, 0)[:, 0, :]), BANK, S)
+        weave_x(1, 3)
         round_three(1)
         fetch(1, 3)
-        regroup_chunk(3, 3)
         store_page(1, 3)
         round_last(0)
         scale_x(1, 3)
         round_last(1)
-        nc.vector.tensor_copy(out=staged(1, 2)[:, 3, :], in_=pages[1, 3][:, 2 * BANK : 3 * BANK])
-        round_planes(1, 2, "vector")
+        nc.vector.tensor_copy(out=stages[1, 1][:, 6 * BANK : 8 * BANK], in_=pages[1, 3][:, 2 * BANK : 4 * BANK])
         planes(1, 0)
+        round_planes(1, 2, "vector")
         quantize_x(1)
         score_pass(1)
         planes(1, 2)
-        round_planes(1, 3, "vector")
         planes(1, 1)
+        round_planes(1, 3, "vector")
         for n in range(3):
-            y = ring.tile([P, M], F32, name=f"y{n}", tag="h_row", bufs=3)
+            y = ring.tile([P, M], F32, name=f"y{n}", tag="h_row", bufs=3, align_bytes=ALIGN)
             nc.scalar.activation(out=y[:], in_=scores[n][:], func=ACT.Square)
             nc.sync.dma_start(out=out_0[P * n : P * (n + 1), :], in_=y[:])
         planes(1, 3)

@@ -131,9 +131,9 @@ def tile_list_linen_soil_slots_kernel(
         v_plane_moved = keep.tile([P, S], U8, name="v_plane_moved", align_bytes=ALIGN)
         nc.vector.memset(v_plane_moved[:].bitcast(I32), 0)
         nc.vector.tensor_copy(v_plane[:], tab_plane[:].indirect(list1[:]))
+        tabs.append(load_tab(1))
         for r in range(4):
             nc.sync.dma_start(out=v_plane_moved[r:P:32, :].bitcast(I32), in_=v_plane[4 + r : P : 32, :].bitcast(I32))
-        tabs.append(load_tab(1))
         nc.sync.dma_start(list2[:], offs2)
         for t in range(PACK):
             load_page(0, t)
@@ -320,7 +320,7 @@ def tile_list_linen_soil_slots_kernel(
         rounded = {}
 
         def round_planes(g, c, engine):
-            rounded[g, c] = late([P, BANK, PACK], BF16, f"ybf{g}{c}")
+            rounded[g, c] = late([P, BANK, PACK], BF16, f"ybf{g}{c}") if (g, c) != (1, 3) else rounded[1, 1]
             interleave(engine, rounded[g, c][:], staged(g, c))
 
         def round_three(c):
@@ -348,17 +348,13 @@ def tile_list_linen_soil_slots_kernel(
         w3_codes = keep.tile([P, 2 * N], U32, name="w3_codes", align_bytes=ALIGN)
         w3_plane = keep.tile([P, 2 * N], U8, name="w3_plane", align_bytes=ALIGN)
 
-        def quantize_w3(g):
-            if g == 0:
-                grouped = unit_tile([P, N, PACK], BF16, 0, 3, "w3bf0")
-            else:
-                grouped = relay([P, N, PACK], BF16, "w3bf1")
-            interleave(("scalar", "vector")[g], grouped[:], w3_raw[g])
-            for c0, c1 in ((0, 256), (256, N)):
-                quantize(
-                    w3_codes[:, N * g + c0 : N * g + c1], w3_plane[:, N * g + c0 : N * g + c1],
-                    grouped[:, c0:c1, :].rearrange("p c t -> p (c t)"),
-                )
+        def quantize_w3():
+            grouped = relay([P, 2 * N * PACK], BF16, "w3bf")
+            for g in range(2):
+                part = grouped[:, g * N * PACK : (g + 1) * N * PACK]
+                interleave("scalar", part.rearrange("p (c t) -> p c t", t=PACK), w3_raw[g])
+            for c0, c1 in ((0, BANK), (BANK, 2 * N)):
+                quantize(w3_codes[:, c0:c1], w3_plane[:, c0:c1], grouped[:, PACK * c0 : PACK * c1])
 
         scores = {}
 
@@ -381,8 +377,7 @@ def tile_list_linen_soil_slots_kernel(
             store_page(0, t)
         quantize_w1(1)
         scatter_last_tile(last_banks)
-        quantize_w3(0)
-        quantize_w3(1)
+        quantize_w3()
         picked_rows = relay([P, PACK * M], F32, "picked_rows")
         for t in range(PACK):
             fetch(0, t, picked_rows[:, M * t : M * (t + 1)])

@@ -50,20 +50,11 @@ def tile_list_linen_soil_slots_kernel(
         def unit_tile(shape, dtype, side, q, name):
             return ring.tile(shape, dtype, name=name, tag=f"unit{side}{q}", bufs=1, align_bytes=ALIGN)
 
-        def interleave(engine, dst, src):
-            d = dst.rearrange("p (c i) t -> p c t i", i=2)
-            s = src.rearrange("p t (c i) -> p c t i", i=2)
-            if engine == "scalar":
-                nc.scalar.copy(out=d, in_=s)
-            else:
-                nc.vector.tensor_copy(out=d, in_=s)
+        def interleave(copy, dst, src):
+            copy(out=dst.rearrange("p (c i) t -> p c t i", i=2), in_=src.rearrange("p t (c i) -> p c t i", i=2))
 
-        def scale_rows(queue, plane, scales):
-            for r in range(4):
-                queue.dma_start(
-                    out=plane[r:P:32, :].bitcast(I32).rearrange("p (a c) -> p a c", a=2),
-                    in_=scales[:, r:16:4, :].rearrange("a q c -> q a c").bitcast(I32),
-                )
+        def quantize(codes, plane, grouped):
+            nc.vector.quantize_mx(out=codes.bitcast(FP8X4), scales=plane, in_=grouped)
 
         list1 = keep.tile([P, S // 16], U16, name="list1")
         list2 = keep.tile([P, S // 16], U16, name="list2")
@@ -74,7 +65,11 @@ def tile_list_linen_soil_slots_kernel(
         nc.vector.memset(w2_plane[:].bitcast(I32), 0)
         ident = keep.tile([P, P], F32, name="ident")
         make_identity(nc, ident[:])
-        scale_rows(nc.gpsimd, w2_plane, w2_scales)
+        for r in range(4):
+            nc.gpsimd.dma_start(
+                out=w2_plane[r:P:32, :].bitcast(I32).rearrange("p (a c) -> p a c", a=2),
+                in_=w2_scales[:, r:16:4, :].rearrange("a q c -> q a c").bitcast(I32),
+            )
         gains = keep.tile([P, 2, PACK], F32, name="gains")
         svs = keep.tile([P, 2, PACK], F32, name="svs")
         nc.gpsimd.dma_start(out=gains[:], in_=gain.rearrange("(g p t) -> p g t", g=2, t=PACK))
@@ -97,7 +92,10 @@ def tile_list_linen_soil_slots_kernel(
             return words
 
         v_codes = [late([P, S], U32, f"v_codes{a}") for a in range(2)]
-        w2_codes = [keep.tile([P, 2, 2 * PASS], U8, name="w2_codes0", align_bytes=ALIGN), late([P, 2, 2 * PASS], U8, "w2_codes1")]
+        w2_codes = [
+            keep.tile([P, 2, 2 * PASS], U8, name="w2_codes0", align_bytes=ALIGN),
+            late([P, 2, 2 * PASS], U8, "w2_codes1"),
+        ]
 
         def load_w2(g):
             nc.sync.dma_start(
@@ -159,9 +157,10 @@ def tile_list_linen_soil_slots_kernel(
                 nc.tensor.transpose(bank[:, b, :], wgs_rows[:, P * jb : P * (jb + 1)], ident[:])
             for e in range(2):
                 repeated[u, e] = unit_tile([P, 2, PACK, P], F32, e, 2 + u, f"wgs_repeated{u}{e}")
+                rows = bank[:, 2 * e : 2 * e + 2, :].rearrange("j b (k v t) -> j b t k v", k=1, t=PACK)
                 nc.scalar.copy(
-                    out=repeated[u, e][:].rearrange("j b t (k v) -> j b k v t", k=4),
-                    in_=bank[:, 2 * e : 2 * e + 2, :].rearrange("j b (k v t) -> j b k v t", k=1, t=PACK).to_broadcast([P, 2, 4, 32, PACK]),
+                    out=repeated[u, e][:].rearrange("j b t (k v) -> j b t k v", k=4),
+                    in_=rows.to_broadcast([P, 2, PACK, 4, 32]),
                 )
 
         def deal_weights(u):
@@ -171,45 +170,46 @@ def tile_list_linen_soil_slots_kernel(
                     nc.tensor.transpose(bank[:, P * b : P * (b + 1)], repeated[u, b // 2][:, b % 2, t, :], ident[:])
                 nc.scalar.copy(out=weights[:, t, BANK * u : BANK * (u + 1)], in_=bank[:])
 
-        w1_codes = [keep.tile([P, 2 * BANK], U32, name="w1_codes0", align_bytes=ALIGN), late([P, 2 * BANK], U32, "w1_codes1")]
+        w1_codes = [
+            keep.tile([P, 2 * BANK], U32, name="w1_codes0", align_bytes=ALIGN),
+            late([P, 2 * BANK], U32, "w1_codes1"),
+        ]
         w1_plane = keep.tile([P, 4 * BANK], U8, name="w1_plane", align_bytes=ALIGN)
 
-        def quantize(codes, plane, grouped):
-            nc.vector.quantize_mx(out=codes.bitcast(FP8X4), scales=plane, in_=grouped)
+        def words_of(flat):
+            return flat.rearrange("p (c t) -> p c t", t=PACK)
 
-        def quantize_w1(g):
-            grouped = relay([P, 2 * BANK * PACK], BF16, f"w1bf{g}")
-            for a in range(2):
-                part = grouped[:, a * BANK * PACK : (a + 1) * BANK * PACK]
-                interleave("vector" if g == 0 else "scalar", part.rearrange("p (c t) -> p c t", t=PACK), w1_raw[g, a])
-                if g == 0:
-                    quantize(w1_codes[0][:, a * BANK : (a + 1) * BANK], w1_plane[:, a * BANK : (a + 1) * BANK], part)
-            if g == 1:
-                quantize(w1_codes[1][:], w1_plane[:, 2 * BANK : 4 * BANK], grouped[:])
-
-        def gather_words(a, j0, j1):
-            nc.vector.tensor_copy(v_codes[a][:, j0:j1], tabs[a].indirect(list1[:, j0 // 16 : j1 // 16]))
-
-        quantize_w1(0)
+        w1_grouped = relay([P, 2 * BANK * PACK], BF16, "w1bf0")
+        for a in range(2):
+            part = w1_grouped[:, a * BANK * PACK : (a + 1) * BANK * PACK]
+            interleave(nc.vector.tensor_copy, words_of(part), w1_raw[0, a])
+            quantize(w1_codes[0][:, a * BANK : (a + 1) * BANK], w1_plane[:, a * BANK : (a + 1) * BANK], part)
         deal_weights(1)
         deal_weights(0)
         for j0, j1 in ((0, QUARTER), (QUARTER, S)):
             for a in range(2):
-                gather_words(a, j0, j1)
+                nc.vector.tensor_copy(v_codes[a][:, j0:j1], tabs[a].indirect(list1[:, j0 // 16 : j1 // 16]))
+
+        def quantize_second_w1():
+            grouped = relay([P, 2 * BANK * PACK], BF16, "w1bf1")
+            for a in range(2):
+                interleave(nc.scalar.copy, words_of(grouped[:, a * BANK * PACK : (a + 1) * BANK * PACK]), w1_raw[1, a])
+            quantize(w1_codes[1][:], w1_plane[:, 2 * BANK : 4 * BANK], grouped[:])
 
         mags = {}
 
         def magnitudes(g, jb):
+            q = jb // 2
             if (g, jb) == (0, 2):
                 both = relay([P, 2, 2, PACK, P], F32, "mag_unit1")
-                mags[0, 1], mags[1, 1] = both[:, 0], both[:, 1]
+                mags[0, q], mags[1, q] = both[:, 0], both[:, 1]
             elif jb % 2 == 0:
                 for side in range(2):
-                    mags[side, jb // 2] = unit_tile([P, 2, PACK, P], F32, side, jb // 2, f"mag{g}{side}{jb // 2}")
-            mag_a = mags[0, jb // 2][:, jb % 2]
-            neg_b = mags[1, jb // 2][:, jb % 2]
+                    mags[side, q] = unit_tile([P, 2, PACK, P], F32, side, q, f"mag{g}{side}{q}")
+            mag_a = mags[0, q][:, jb % 2]
+            neg_b = mags[1, q][:, jb % 2]
             js = slice(P * jb, P * (jb + 1))
-            first = 4 if g == 0 and jb >= 2 else 0
+            first = 4 if g == 0 and q > 0 else 0
             acc_a = bank_tile([P, BANK], first + 2 * (jb % 2), "acc_a")
             acc_b = bank_tile([P, BANK], first + 2 * (jb % 2) + 1, "acc_b")
             for a in range(2):
@@ -219,124 +219,121 @@ def tile_list_linen_soil_slots_kernel(
                     rhs_scale=w2_plane[:, a * H + PASS * g : a * H + PASS * (g + 1)], start=(a == 0), stop=(a == 1),
                 )
             for a in range(2):
-                cols = slice((2 * g + a) * BANK, (2 * g + a + 1) * BANK)
                 nc.tensor.matmul_mx(
                     out=acc_a[:], lhsT=v_codes[a][:, js].bitcast(FP8X4), lhsT_scale=v_plane[4 * a : P, js],
-                    rhs=w1_codes[g][:, a * BANK : (a + 1) * BANK].bitcast(FP8X4), rhs_scale=w1_plane[:, cols], start=(a == 0), stop=(a == 1),
+                    rhs=w1_codes[g][:, a * BANK : (a + 1) * BANK].bitcast(FP8X4),
+                    rhs_scale=w1_plane[:, (2 * g + a) * BANK : (2 * g + a + 1) * BANK], start=(a == 0), stop=(a == 1),
                 )
             for mag, acc in ((neg_b, acc_b), (mag_a, acc_a)):
-                nc.scalar.activation(
-                    out=mag.rearrange("j t p -> j p t"), in_=acc[:].rearrange("j (p t) -> j p t", t=PACK), func=ACT.Abs
-                )
-            if g == 0 and jb < 2:
+                nc.scalar.activation(out=mag, in_=acc[:].rearrange("j (p t) -> j t p", t=PACK), func=ACT.Abs)
+            if (g, q) == (0, 0):
                 nc.vector.tensor_scalar_mul(out=neg_b, in0=neg_b, scalar1=-1.0)
-            else:
-                nc.scalar.activation(out=neg_b, in_=neg_b, func=ACT.Copy, scale=-1.0)
+            elif jb % 2 == 1:
+                nc.scalar.activation(out=mags[1, q][:], in_=mags[1, q][:], func=ACT.Copy, scale=-1.0)
 
-        def turn(bank, t, jb):
-            nc.tensor.matmul(out=bank, lhsT=mags[1, jb // 2][:, jb % 2, t, :], rhs=ident[:], is_transpose=True, start=True, stop=False)
-            nc.tensor.matmul(out=bank, lhsT=mags[0, jb // 2][:, jb % 2, t, :], rhs=ident[:], is_transpose=True, start=False, stop=True)
+        def turn(dst, t, jb):
+            for side in (1, 0):
+                nc.tensor.matmul(
+                    out=dst, lhsT=mags[side, jb // 2][:, jb % 2, t, :], rhs=ident[:], is_transpose=True,
+                    start=(side == 1), stop=(side == 0),
+                )
+
+        def apply_gain(h, bank, g, t):
+            nc.scalar.activation(out=h, in_=bank[:], func=ACT.Copy, scale=gains[:, g, t : t + 1])
 
         def scatter(g, t, h, j0, j1):
             nc.vector.tensor_tensor(
                 pages[g, t][:].indirect(list2[:, j0 // 16 : j1 // 16]), h, weights[:, t, j0:j1], MULT
             )
 
-        def quarter_unit(q):
-            for t in range(PACK if q < 2 else PACK - 1):
+        def scatter_quarter(q, tiles):
+            for t in range(tiles):
                 bank = bank_tile([P, QUARTER], (4 if q == 0 else 0) + t, "turned")
                 for b in range(2):
                     turn(bank[:, P * b : P * (b + 1)], t, 2 * q + b)
                 h = ring.tile([P, QUARTER], F32, name="h_quarter", tag="h_quarter", bufs=7)
-                nc.scalar.activation(out=h[:], in_=bank[:], func=ACT.Copy, scale=gains[:, 0, t : t + 1])
+                apply_gain(h[:], bank, 0, t)
                 scatter(0, t, h[:], QUARTER * q, QUARTER * (q + 1))
 
-        def turn_last_tile():
-            bank = bank_tile([P, BANK], 3, "turned")
-            for b in range(4):
-                turn(bank[:, P * b : P * (b + 1)], 3, 4 + b)
-            return bank
-
-        def scatter_last_tile(bank):
-            h = w1_tiles[1][:, PACK * BANK : PACK * BANK + BANK]
-            nc.scalar.activation(out=h, in_=bank[:], func=ACT.Copy, scale=gains[:, 0, 3:4])
-            scatter(0, 3, h, BANK, S)
-
         h_rows = {}
-        next_bank = [0, 1, 2, 3, 0, 1, 2, 3]
+        halves_turned = []
 
-        def half_row(t, u, h=None):
+        def half_row(t, u):
             if u == 0:
                 h_rows[t] = ring.tile([P, S], F32, name=f"h_row{t}", tag="h_row", bufs=3, align_bytes=ALIGN)
-            if h is None:
-                h = h_rows[t][:, BANK * u : BANK * (u + 1)]
-            bank = bank_tile([P, BANK], 4 + next_bank.pop(0), "turned")
+            h = h_rows[t][:, BANK * u : BANK * (u + 1)]
+            bank = bank_tile([P, BANK], 4 + len(halves_turned) % 4, "turned")
+            halves_turned.append((t, u))
             for b in range(4):
                 turn(bank[:, P * b : P * (b + 1)], t, 4 * u + b)
-            nc.scalar.activation(out=h, in_=bank[:], func=ACT.Copy, scale=gains[:, 1, t : t + 1])
+            apply_gain(h, bank, 1, t)
             return h
 
         x_codes = [keep.tile([P, M], U32, name=f"x_codes{g}", align_bytes=ALIGN) for g in range(2)]
         x_plane = [keep.tile([P, M], U8, name=f"x_plane{g}", align_bytes=ALIGN) for g in range(2)]
-        x_tiles = {}
+        x_words = {}
         x_rows = {}
         picked = {}
 
-        def fetch(g, t, dst=None):
-            picked[g, t] = ring.tile([P, M], F32, name="picked", tag="picked", bufs=3)[:] if dst is None else dst
-            nc.vector.tensor_copy(picked[g, t], pages[g, t][:].indirect(list3[:]))
+        def fetch(g, t, dst):
+            picked[g, t] = dst
+            nc.vector.tensor_copy(dst, pages[g, t][:].indirect(list3[:]))
 
-        def scale_x(g, t):
-            if t == 0:
-                x_rows[g] = late([P, PACK, M], BF16, f"x_rows{g}")
-            dst = x_tiles[1][:, :, 3] if (g, t) == (1, 3) else x_rows[g][:, t, :]
+        def fetch_late(t):
+            fetch(1, t, ring.tile([P, M], F32, name="picked", tag="picked", bufs=3)[:])
+
+        def scale_x(g, t, dst):
             nc.scalar.activation(out=dst, in_=picked[g, t], func=ACT.Copy, scale=svs[:, g, t : t + 1])
 
-        def weave_x(g, rows):
-            x_tiles[g] = (relay, late)[g]([P, M, PACK], BF16, f"xbf{g}")
-            interleave("scalar", x_tiles[g][:, :, 0:rows], x_rows[g][:, 0:rows, :])
+        def scale_x_row(g, t):
+            if t == 0:
+                x_rows[g] = late([P, PACK, M], BF16, f"x_rows{g}")
+            scale_x(g, t, x_rows[g][:, t, :])
+
+        def weave_x(g, rows, place):
+            x_words[g] = place([P, M, PACK], BF16, f"xbf{g}")
+            interleave(nc.scalar.copy, x_words[g][:, :, 0:rows], x_rows[g][:, 0:rows, :])
 
         def quantize_x(g):
-            quantize(x_codes[g][:], x_plane[g][:], x_tiles[g][:].rearrange("p c t -> p (c t)"))
+            quantize(x_codes[g][:], x_plane[g][:], x_words[g][:].rearrange("p c t -> p (c t)"))
 
         def store_page(g, t):
             nc.sync.dma_start(out=page_out[g, t], in_=pages[g, t][:])
 
         stages = {}
 
-        def staged(g, c):
-            tile = stages[g, c // 2][:].rearrange("p (t m) -> p t m", t=PACK)
-            return tile[:, :, BANK * (c % 2) : BANK * (c % 2 + 1)]
-
         def regroup(g, t, u):
-            if (g, u) not in stages:
+            if t == 0:
                 stages[g, u] = wide([P, PACK * 2 * BANK], F32, u, f"stage{g}{u}")
             nc.sync.dma_start(
-                out=stages[g, u][:, 2 * BANK * t : 2 * BANK * (t + 1)], in_=pages[g, t][:, 2 * BANK * u : 2 * BANK * (u + 1)]
+                out=stages[g, u][:, 2 * BANK * t : 2 * BANK * (t + 1)],
+                in_=pages[g, t][:, 2 * BANK * u : 2 * BANK * (u + 1)],
             )
 
-        y_planes = [keep.tile([P, T2], U8, name=f"y_plane{g}", align_bytes=ALIGN) for g in range(2)]
+        def staged(g, c):
+            rows = stages[g, c // 2][:].rearrange("p (t m) -> p t m", t=PACK)
+            return rows[:, :, BANK * (c % 2) : BANK * (c % 2 + 1)]
 
+        y_planes = [keep.tile([P, T2], U8, name=f"y_plane{g}", align_bytes=ALIGN) for g in range(2)]
         rounded = {}
 
-        def round_planes(g, c, engine):
-            rounded[g, c] = late([P, BANK, PACK], BF16, f"ybf{g}{c}") if (g, c) != (1, 3) else rounded[1, 1]
-            interleave(engine, rounded[g, c][:], staged(g, c))
+        def round_chunk(g, c, copy):
+            rounded[g, c] = late([P, BANK, PACK], BF16, f"ybf{g}{c}")
+            interleave(copy, rounded[g, c][:], staged(g, c))
 
         def round_three(c):
             if c == 0:
                 rounded["pair"] = relay([P, 2 * BANK * PACK], BF16, "ybf1pair")
-            rounded[1, c] = rounded["pair"][:, BANK * PACK * c : BANK * PACK * (c + 1)].rearrange("p (c t) -> p c t", t=PACK)
-            interleave("scalar", rounded[1, c][:, :, 0:3], staged(1, c)[:, 0:3, :])
+            rounded[1, c] = words_of(rounded["pair"][:, BANK * PACK * c : BANK * PACK * (c + 1)])
+            interleave(nc.scalar.copy, rounded[1, c][:, :, 0:3], staged(1, c)[:, 0:3, :])
 
         def round_last(c):
             nc.scalar.copy(out=rounded[1, c][:, :, 3], in_=pages[1, 3][:, BANK * c : BANK * (c + 1)])
 
-        def planes(g, c):
+        def quantize_chunk(g, c):
             cols = slice(BANK * c, BANK * (c + 1))
-            grouped = rounded[g, c]
             codes = ring.tile([P, BANK], U32, name="y_codes", tag="y_codes", bufs=6, align_bytes=ALIGN)
-            quantize(codes[:], y_planes[g][:, cols], grouped[:].rearrange("p c t -> p (c t)"))
+            quantize(codes[:], y_planes[g][:, cols], rounded[g, c][:].rearrange("p c t -> p (c t)"))
             nc.sync.dma_start(
                 out=out_2[g, :, cols, :].rearrange("p m t -> p (m t)").bitcast(I32), in_=codes[:].bitcast(I32)
             )
@@ -351,15 +348,14 @@ def tile_list_linen_soil_slots_kernel(
         def quantize_w3():
             grouped = relay([P, 2 * N * PACK], BF16, "w3bf")
             for g in range(2):
-                part = grouped[:, g * N * PACK : (g + 1) * N * PACK]
-                interleave("scalar", part.rearrange("p (c t) -> p c t", t=PACK), w3_raw[g])
+                interleave(nc.scalar.copy, words_of(grouped[:, g * N * PACK : (g + 1) * N * PACK]), w3_raw[g])
             for c0, c1 in ((0, BANK), (BANK, 2 * N)):
                 quantize(w3_codes[:, c0:c1], w3_plane[:, c0:c1], grouped[:, PACK * c0 : PACK * c1])
 
         scores = {}
 
         def score_pass(g):
-            for n in range(3):
+            for n in range(N // P):
                 if g == 0:
                     scores[n] = bank_tile([P, M], n, f"score{n}")
                 cols = slice(N * g + P * n, N * g + P * (n + 1))
@@ -371,12 +367,16 @@ def tile_list_linen_soil_slots_kernel(
         for q in range(4):
             magnitudes(0, 2 * q)
             magnitudes(0, 2 * q + 1)
-            quarter_unit(q)
-        last_banks = turn_last_tile()
+            scatter_quarter(q, PACK if q < 2 else PACK - 1)
+        last_bank = bank_tile([P, BANK], 3, "turned")
+        for b in range(4):
+            turn(last_bank[:, P * b : P * (b + 1)], 3, 4 + b)
         for t in range(3):
             store_page(0, t)
-        quantize_w1(1)
-        scatter_last_tile(last_banks)
+        quantize_second_w1()
+        last_h = w1_tiles[1][:, PACK * BANK : PACK * BANK + BANK]
+        apply_gain(last_h, last_bank, 0, 3)
+        scatter(0, 3, last_h, BANK, S)
         quantize_w3()
         picked_rows = relay([P, PACK * M], F32, "picked_rows")
         for t in range(PACK):
@@ -392,17 +392,17 @@ def tile_list_linen_soil_slots_kernel(
             for t in range(3 - u):
                 scatter(1, t, half_row(t, u), BANK * u, BANK * (u + 1))
         for t in range(PACK):
-            scale_x(0, t)
-        fetch(1, 0)
-        fetch(1, 1)
+            scale_x_row(0, t)
+        fetch_late(0)
+        fetch_late(1)
         store_page(1, 0)
         scatter(1, 2, half_row(2, 1), BANK, S)
-        fetch(1, 2)
-        round_planes(0, 0, "scalar")
-        round_planes(0, 1, "scalar")
-        weave_x(0, PACK)
-        round_planes(0, 2, "scalar")
-        round_planes(0, 3, "scalar")
+        fetch_late(2)
+        round_chunk(0, 0, nc.scalar.copy)
+        round_chunk(0, 1, nc.scalar.copy)
+        weave_x(0, PACK, relay)
+        round_chunk(0, 2, nc.scalar.copy)
+        round_chunk(0, 3, nc.scalar.copy)
         regroup(1, 0, 0)
         regroup(1, 1, 0)
         store_page(1, 1)
@@ -410,37 +410,38 @@ def tile_list_linen_soil_slots_kernel(
         store_page(1, 2)
         for t in range(3):
             regroup(1, t, 1)
-        planes(0, 0)
-        planes(0, 1)
+        quantize_chunk(0, 0)
+        quantize_chunk(0, 1)
         quantize_x(0)
         score_pass(0)
-        planes(0, 2)
-        planes(0, 3)
+        quantize_chunk(0, 2)
+        quantize_chunk(0, 3)
         store_scales(0)
-        half_row(3, 0)
-        half_row(3, 1)
-        scatter(1, 3, h_rows[3][:], 0, S)
+        scatter(1, 3, half_row(3, 0), 0, BANK)
         for t in range(3):
-            scale_x(1, t)
+            scale_x_row(1, t)
+        scatter(1, 3, half_row(3, 1), BANK, S)
+        weave_x(1, 3, late)
         round_three(0)
-        weave_x(1, 3)
         round_three(1)
-        fetch(1, 3)
+
+        fetch_late(3)
         store_page(1, 3)
         round_last(0)
-        scale_x(1, 3)
+        scale_x(1, 3, x_words[1][:, :, 3])
         round_last(1)
         nc.vector.tensor_copy(out=stages[1, 1][:, 6 * BANK : 8 * BANK], in_=pages[1, 3][:, 2 * BANK : 4 * BANK])
-        planes(1, 0)
-        round_planes(1, 2, "vector")
+        quantize_chunk(1, 0)
+        round_chunk(1, 2, nc.vector.tensor_copy)
         quantize_x(1)
         score_pass(1)
-        planes(1, 2)
-        planes(1, 1)
-        round_planes(1, 3, "vector")
-        for n in range(3):
+        quantize_chunk(1, 2)
+        quantize_chunk(1, 1)
+        rounded[1, 3] = rounded[1, 1]
+        interleave(nc.vector.tensor_copy, rounded[1, 3][:], staged(1, 3))
+        for n in range(N // P):
             y = ring.tile([P, M], F32, name=f"y{n}", tag="h_row", bufs=3, align_bytes=ALIGN)
             nc.scalar.activation(out=y[:], in_=scores[n][:], func=ACT.Square)
             nc.sync.dma_start(out=out_0[P * n : P * (n + 1), :], in_=y[:])
-        planes(1, 3)
+        quantize_chunk(1, 3)
         store_scales(1)

from contextlib import ExitStack

import concourse.mybir as mybir
from concourse.masks import make_identity

K, H, N, T, S, T2, M = 1024, 1024, 384, 2048, 1024, 2048, 512
FLOPS = 2 * 2 * K * H * S + 2 * H * N * M

F32 = mybir.dt.float32
BF16 = mybir.dt.bfloat16
I32 = mybir.dt.int32
U32 = mybir.dt.uint32
U16 = mybir.dt.uint16
U8 = mybir.dt.uint8
FP8X4 = mybir.dt.float8_e4m3fn_x4
FP4X4 = mybir.dt.float4_e2m1fn_x4
ACT = mybir.ActivationFunctionType
MULT = mybir.AluOpType.mult

P = 128
PACK = 4
PASS = P * PACK
BANK = 512
QUARTER = 256
ALIGN = 256


def tile_list_linen_soil_slots_kernel(
    tc, tab_words, tab_scales, offs, offs2, offs3, w1, w2_words, w2_scales, gain, wgs, page0, sv, w3,
    out_0, out_1, out_2, out_3,
):
    nc = tc.nc
    with ExitStack() as ctx:
        keep = ctx.enter_context(tc.tile_pool(name="keep", bufs=1))
        ring = ctx.enter_context(tc.tile_pool(name="ring", bufs=1))
        psum = ctx.enter_context(tc.psum_pool(name="psum", bufs=1))

        def wide(shape, dtype, side, name):
            return ring.tile(shape, dtype, name=name, tag=f"wide{side}", bufs=1, align_bytes=ALIGN)

        def relay(shape, dtype, name):
            return ring.tile(shape, dtype, name=name, tag="relay", bufs=1, align_bytes=ALIGN)

        def late(shape, dtype, name):
            return ring.tile(shape, dtype, name=name, tag="late", bufs=4, align_bytes=ALIGN)

        def bank_tile(shape, n, name):
            return psum.tile(shape, F32, name=name, tag=f"bank{n}", bufs=1)

        def unit_tile(shape, dtype, side, q, name):
            return ring.tile(shape, dtype, name=name, tag=f"unit{side}{q}", bufs=1, align_bytes=ALIGN)

        def interleave(copy, dst, src):
            copy(out=dst.rearrange("p (c i) t -> p c t i", i=2), in_=src.rearrange("p t (c i) -> p c t i", i=2))

        def quantize(codes, plane, grouped):
            nc.vector.quantize_mx(out=codes.bitcast(FP8X4), scales=plane, in_=grouped)

        list1 = keep.tile([P, S // 16], U16, name="list1")
        list2 = keep.tile([P, S // 16], U16, name="list2")
        list3 = keep.tile([P, M // 16], U16, name="list3")
        tab_plane = keep.tile([P, T], U8, name="tab_plane", align_bytes=ALIGN)
        w2_plane = keep.tile([P, 2 * H], U8, name="w2_plane", align_bytes=ALIGN)
        nc.vector.memset(tab_plane[:].bitcast(I32), 0)
        nc.vector.memset(w2_plane[:].bitcast(I32), 0)
        ident = keep.tile([P, P], F32, name="ident")
        make_identity(nc, ident[:])
        for r in range(4):
            nc.gpsimd.dma_start(
                out=w2_plane[r:P:32, :].bitcast(I32).rearrange("p (a c) -> p a c", a=2),
                in_=w2_scales[:, r:16:4, :].rearrange("a q c -> q a c").bitcast(I32),
            )
        gains = keep.tile([P, 2, PACK], F32, name="gains")
        svs = keep.tile([P, 2, PACK], F32, name="svs")
        nc.gpsimd.dma_start(out=gains[:], in_=gain.rearrange("(g p t) -> p g t", g=2, t=PACK))

        w1_tiles = {}

        def load_w1(g, a):
            if a == 0:
                w1_tiles[g] = wide([P, 2 * PACK * BANK], F32, 1, f"w1raw{g}")
            raw = w1_tiles[g][:, PACK * BANK * a : PACK * BANK * (a + 1)].rearrange("p (i c) -> p i c", i=PACK)
            nc.sync.dma_start(
                out=raw,
                in_=w1[PASS * a : PASS * (a + 1), PASS * g : PASS * (g + 1)].rearrange("(p i) c -> p i c", i=PACK),
            )
            return raw

        def load_tab(a):
            words = tab_tile[:, T * a : T * (a + 1)]
            nc.sync.dma_start(out=words.bitcast(I32), in_=tab_words[a].rearrange("p t i -> p (t i)").bitcast(I32))
            return words

        v_codes = [late([P, S], U32, f"v_codes{a}") for a in range(2)]
        w2_codes = [
            keep.tile([P, 2, 2 * PASS], U8, name="w2_codes0", align_bytes=ALIGN),
            late([P, 2, 2 * PASS], U8, "w2_codes1"),
        ]

        def load_w2(g):
            nc.sync.dma_start(
                out=w2_codes[g][:].bitcast(I32),
                in_=w2_words[:, :, 2 * PASS * g : 2 * PASS * (g + 1)].rearrange("a p c -> p a c").bitcast(I32),
            )

        weights = keep.tile([P, PACK, S], F32, name="weights")

        pages = {}
        page_in = page0.rearrange("(g p t) m -> g t p m", g=2, t=PACK)
        page_out = out_1.rearrange("(g p t) m -> g t p m", g=2, t=PACK)

        def load_page(g, t):
            pages[g, t] = ring.tile([P, T2], F32, name=f"page{g}{t}", tag="page", bufs=8, align_bytes=ALIGN)
            nc.sync.dma_start(out=pages[g, t][:], in_=page_in[g, t])

        wgs_rows = unit_tile([P, S], F32, 0, 1, "wgs_rows")
        nc.sync.dma_start(out=wgs_rows[:], in_=wgs)
        w1_raw = {(0, 0): load_w1(0, 0)}
        for q in range(4):
            nc.sync.dma_start(
                out=tab_plane[32 * q : 32 * q + 8, :].bitcast(I32), in_=tab_scales[:, 4 * q : 4 * q + 4, :].bitcast(I32)
            )
        nc.sync.dma_start(list1[:], offs)
        w1_raw[0, 1] = load_w1(0, 1)
        tab_tile = wide([P, 2 * T], U32, 0, "tab")
        load_w2(0)
        tabs = [load_tab(0)]
        v_plane = keep.tile([P, S], U8, name="v_plane", align_bytes=ALIGN)
        v_plane_moved = keep.tile([P, S], U8, name="v_plane_moved", align_bytes=ALIGN)
        nc.vector.memset(v_plane_moved[:].bitcast(I32), 0)
        nc.vector.tensor_copy(v_plane[:], tab_plane[:].indirect(list1[:]))
        tabs.append(load_tab(1))
        for r in range(4):
            nc.sync.dma_start(out=v_plane_moved[r:P:32, :].bitcast(I32), in_=v_plane[4 + r : P : 32, :].bitcast(I32))
        nc.sync.dma_start(list2[:], offs2)
        for t in range(PACK):
            load_page(0, t)
        w1_raw[1, 0] = load_w1(1, 0)
        w1_raw[1, 1] = load_w1(1, 1)
        w3_raw = []
        w3_tile = wide([P, 2 * PACK * N], F32, 0, "w3raw")
        for g in range(2):
            raw = w3_tile[:, PACK * N * g : PACK * N * (g + 1)].rearrange("p (i n) -> p i n", i=PACK)
            nc.sync.dma_start(out=raw, in_=w3[PASS * g : PASS * (g + 1), :].rearrange("(p i) n -> p i n", i=PACK))
            w3_raw.append(raw)
        load_w2(1)
        nc.sync.dma_start(list3[:], offs3)
        nc.sync.dma_start(out=svs[:], in_=sv.rearrange("(g p t) -> p g t", g=2, t=PACK))
        for t in range(PACK):
            load_page(1, t)

        repeated = {}
        for u in (1, 0):
            bank = bank_tile([P, 4, P], u, "wgs_turned")
            for b in range(4):
                jb = 4 * u + b
                nc.tensor.transpose(bank[:, b, :], wgs_rows[:, P * jb : P * (jb + 1)], ident[:])
            for e in range(2):
                repeated[u, e] = unit_tile([P, 2, PACK, P], F32, e, 2 + u, f"wgs_repeated{u}{e}")
                rows = bank[:, 2 * e : 2 * e + 2, :].rearrange("j b (k v t) -> j b t k v", k=1, t=PACK)
                nc.scalar.copy(
                    out=repeated[u, e][:].rearrange("j b t (k v) -> j b t k v", k=4),
                    in_=rows.to_broadcast([P, 2, PACK, 4, 32]),
                )

        def deal_weights(u):
            for t in range(PACK):
                bank = bank_tile([P, BANK], 4 * (1 - u) + t, "wgs_dealt")
                for b in range(4):
                    nc.tensor.transpose(bank[:, P * b : P * (b + 1)], repeated[u, b // 2][:, b % 2, t, :], ident[:])
                nc.scalar.copy(out=weights[:, t, BANK * u : BANK * (u + 1)], in_=bank[:])

        w1_codes = [
            keep.tile([P, 2 * BANK], U32, name="w1_codes0", align_bytes=ALIGN),
            late([P, 2 * BANK], U32, "w1_codes1"),
        ]
        w1_plane = keep.tile([P, 4 * BANK], U8, name="w1_plane", align_bytes=ALIGN)

        def words_of(flat):
            return flat.rearrange("p (c t) -> p c t", t=PACK)

        w1_grouped = relay([P, 2 * BANK * PACK], BF16, "w1bf0")
        for a in range(2):
            part = w1_grouped[:, a * BANK * PACK : (a + 1) * BANK * PACK]
            interleave(nc.vector.tensor_copy, words_of(part), w1_raw[0, a])
            quantize(w1_codes[0][:, a * BANK : (a + 1) * BANK], w1_plane[:, a * BANK : (a + 1) * BANK], part)
        deal_weights(1)
        deal_weights(0)
        for j0, j1 in ((0, QUARTER), (QUARTER, S)):
            for a in range(2):
                nc.vector.tensor_copy(v_codes[a][:, j0:j1], tabs[a].indirect(list1[:, j0 // 16 : j1 // 16]))

        def quantize_second_w1():
            grouped = relay([P, 2 * BANK * PACK], BF16, "w1bf1")
            for a in range(2):
                interleave(nc.scalar.copy, words_of(grouped[:, a * BANK * PACK : (a + 1) * BANK * PACK]), w1_raw[1, a])
            quantize(w1_codes[1][:], w1_plane[:, 2 * BANK : 4 * BANK], grouped[:])

        mags = {}

        def magnitudes(g, jb):
            q = jb // 2
            if (g, jb) == (0, 2):
                both = relay([P, 2, 2, PACK, P], F32, "mag_unit1")
                mags[0, q], mags[1, q] = both[:, 0], both[:, 1]
            elif jb % 2 == 0:
                for side in range(2):
                    mags[side, q] = unit_tile([P, 2, PACK, P], F32, side, q, f"mag{g}{side}{q}")
            mag_a = mags[0, q][:, jb % 2]
            neg_b = mags[1, q][:, jb % 2]
            js = slice(P * jb, P * (jb + 1))
            first = 4 if g == 0 and q > 0 else 0
            acc_a = bank_tile([P, BANK], first + 2 * (jb % 2), "acc_a")
            acc_b = bank_tile([P, BANK], first + 2 * (jb % 2) + 1, "acc_b")
            for a in range(2):
                nc.tensor.matmul_mx(
                    out=acc_b[:], lhsT=v_codes[a][:, js].bitcast(FP8X4), lhsT_scale=(v_plane, v_plane_moved)[a][:, js],
                    rhs=w2_codes[g][:, a, :].bitcast(FP4X4),
                    rhs_scale=w2_plane[:, a * H + PASS * g : a * H + PASS * (g + 1)], start=(a == 0), stop=(a == 1),
                )
            for a in range(2):
                nc.tensor.matmul_mx(
                    out=acc_a[:], lhsT=v_codes[a][:, js].bitcast(FP8X4), lhsT_scale=v_plane[4 * a : P, js],
                    rhs=w1_codes[g][:, a * BANK : (a + 1) * BANK].bitcast(FP8X4),
                    rhs_scale=w1_plane[:, (2 * g + a) * BANK : (2 * g + a + 1) * BANK], start=(a == 0), stop=(a == 1),
                )
            for mag, acc in ((neg_b, acc_b), (mag_a, acc_a)):
                nc.scalar.activation(out=mag, in_=acc[:].rearrange("j (p t) -> j t p", t=PACK), func=ACT.Abs)
            if (g, q) == (0, 0):
                nc.vector.tensor_scalar_mul(out=neg_b, in0=neg_b, scalar1=-1.0)
            elif jb % 2 == 1:
                nc.scalar.activation(out=mags[1, q][:], in_=mags[1, q][:], func=ACT.Copy, scale=-1.0)

        def turn(dst, t, jb):
            for side in (1, 0):
                nc.tensor.matmul(
                    out=dst, lhsT=mags[side, jb // 2][:, jb % 2, t, :], rhs=ident[:], is_transpose=True,
                    start=(side == 1), stop=(side == 0),
                )

        def apply_gain(h, bank, g, t):
            nc.scalar.activation(out=h, in_=bank[:], func=ACT.Copy, scale=gains[:, g, t : t + 1])

        def scatter(g, t, h, j0, j1):
            nc.vector.tensor_tensor(
                pages[g, t][:].indirect(list2[:, j0 // 16 : j1 // 16]), h, weights[:, t, j0:j1], MULT
            )

        def scatter_quarter(q, tiles):
            for t in range(tiles):
                bank = bank_tile([P, QUARTER], (4 if q == 0 else 0) + t, "turned")
                for b in range(2):
                    turn(bank[:, P * b : P * (b + 1)], t, 2 * q + b)
                h = ring.tile([P, QUARTER], F32, name="h_quarter", tag="h_quarter", bufs=7)
                apply_gain(h[:], bank, 0, t)
                scatter(0, t, h[:], QUARTER * q, QUARTER * (q + 1))

        h_rows = {}
        halves_turned = []

        def half_row(t, u):
            if u == 0:
                h_rows[t] = ring.tile([P, S], F32, name=f"h_row{t}", tag="h_row", bufs=3, align_bytes=ALIGN)
            h = h_rows[t][:, BANK * u : BANK * (u + 1)]
            bank = bank_tile([P, BANK], 4 + len(halves_turned) % 4, "turned")
            halves_turned.append((t, u))
            for b in range(4):
                turn(bank[:, P * b : P * (b + 1)], t, 4 * u + b)
            apply_gain(h, bank, 1, t)
            return h

        x_codes = [keep.tile([P, M], U32, name=f"x_codes{g}", align_bytes=ALIGN) for g in range(2)]
        x_plane = [keep.tile([P, M], U8, name=f"x_plane{g}", align_bytes=ALIGN) for g in range(2)]
        x_words = {}
        x_rows = {}
        picked = {}

        def fetch(g, t, dst):
            picked[g, t] = dst
            nc.vector.tensor_copy(dst, pages[g, t][:].indirect(list3[:]))

        def fetch_late(t):
            fetch(1, t, ring.tile([P, M], F32, name="picked", tag="picked", bufs=3)[:])

        def scale_x(g, t, dst):
            nc.scalar.activation(out=dst, in_=picked[g, t], func=ACT.Copy, scale=svs[:, g, t : t + 1])

        def scale_x_row(g, t):
            if t == 0:
                x_rows[g] = late([P, PACK, M], BF16, f"x_rows{g}")
            scale_x(g, t, x_rows[g][:, t, :])

        def weave_x(g, rows, place):
            x_words[g] = place([P, M, PACK], BF16, f"xbf{g}")
            interleave(nc.scalar.copy, x_words[g][:, :, 0:rows], x_rows[g][:, 0:rows, :])

        def quantize_x(g):
            quantize(x_codes[g][:], x_plane[g][:], x_words[g][:].rearrange("p c t -> p (c t)"))

        def store_page(g, t):
            nc.sync.dma_start(out=page_out[g, t], in_=pages[g, t][:])

        stages = {}

        def regroup(g, t, u):
            if t == 0:
                stages[g, u] = wide([P, PACK * 2 * BANK], F32, u, f"stage{g}{u}")
            nc.sync.dma_start(
                out=stages[g, u][:, 2 * BANK * t : 2 * BANK * (t + 1)],
                in_=pages[g, t][:, 2 * BANK * u : 2 * BANK * (u + 1)],
            )

        def staged(g, c):
            rows = stages[g, c // 2][:].rearrange("p (t m) -> p t m", t=PACK)
            return rows[:, :, BANK * (c % 2) : BANK * (c % 2 + 1)]

        y_planes = [keep.tile([P, T2], U8, name=f"y_plane{g}", align_bytes=ALIGN) for g in range(2)]
        rounded = {}

        def round_chunk(g, c, copy):
            rounded[g, c] = late([P, BANK, PACK], BF16, f"ybf{g}{c}")
            interleave(copy, rounded[g, c][:], staged(g, c))

        def round_three(c):
            if c == 0:
                rounded["pair"] = relay([P, 2 * BANK * PACK], BF16, "ybf1pair")
            rounded[1, c] = words_of(rounded["pair"][:, BANK * PACK * c : BANK * PACK * (c + 1)])
            interleave(nc.scalar.copy, rounded[1, c][:, :, 0:3], staged(1, c)[:, 0:3, :])

        def round_last(c):
            nc.scalar.copy(out=rounded[1, c][:, :, 3], in_=pages[1, 3][:, BANK * c : BANK * (c + 1)])

        def quantize_chunk(g, c):
            cols = slice(BANK * c, BANK * (c + 1))
            codes = ring.tile([P, BANK], U32, name="y_codes", tag="y_codes", bufs=6, align_bytes=ALIGN)
            quantize(codes[:], y_planes[g][:, cols], rounded[g, c][:].rearrange("p c t -> p (c t)"))
            nc.sync.dma_start(
                out=out_2[g, :, cols, :].rearrange("p m t -> p (m t)").bitcast(I32), in_=codes[:].bitcast(I32)
            )

        def store_scales(g):
            for r in range(4):
                nc.sync.dma_start(out=out_3[g, r:16:4, :].bitcast(I32), in_=y_planes[g][r:P:32, :].bitcast(I32))

        w3_codes = keep.tile([P, 2 * N], U32, name="w3_codes", align_bytes=ALIGN)
        w3_plane = keep.tile([P, 2 * N], U8, name="w3_plane", align_bytes=ALIGN)

        def quantize_w3():
            grouped = relay([P, 2 * N * PACK], BF16, "w3bf")
            for g in range(2):
                interleave(nc.scalar.copy, words_of(grouped[:, g * N * PACK : (g + 1) * N * PACK]), w3_raw[g])
            for c0, c1 in ((0, BANK), (BANK, 2 * N)):
                quantize(w3_codes[:, c0:c1], w3_plane[:, c0:c1], grouped[:, PACK * c0 : PACK * c1])

        scores = {}

        def score_pass(g):
            for n in range(N // P):
                if g == 0:
                    scores[n] = bank_tile([P, M], n, f"score{n}")
                cols = slice(N * g + P * n, N * g + P * (n + 1))
                nc.tensor.matmul_mx(
                    out=scores[n][:], lhsT=w3_codes[:, cols].bitcast(FP8X4), lhsT_scale=w3_plane[:, cols],
                    rhs=x_codes[g][:].bitcast(FP8X4), rhs_scale=x_plane[g][:], start=(g == 0), stop=(g == 1),
                )

        for q in range(4):
            magnitudes(0, 2 * q)
            magnitudes(0, 2 * q + 1)
            scatter_quarter(q, PACK if q < 2 else PACK - 1)
        last_bank = bank_tile([P, BANK], 3, "turned")
        for b in range(4):
            turn(last_bank[:, P * b : P * (b + 1)], 3, 4 + b)
        for t in range(3):
            store_page(0, t)
        quantize_second_w1()
        last_h = w1_tiles[1][:, PACK * BANK : PACK * BANK + BANK]
        apply_gain(last_h, last_bank, 0, 3)
        scatter(0, 3, last_h, BANK, S)
        quantize_w3()
        picked_rows = relay([P, PACK * M], F32, "picked_rows")
        for t in range(PACK):
            fetch(0, t, picked_rows[:, M * t : M * (t + 1)])
        for u in range(2):
            for t in range(PACK):
                regroup(0, t, u)
        store_page(0, 3)

        for u in range(2):
            for jb in range(4 * u, 4 * u + 4):
                magnitudes(1, jb)
            for t in range(3 - u):
                scatter(1, t, half_row(t, u), BANK * u, BANK * (u + 1))
        for t in range(PACK):
            scale_x_row(0, t)
        fetch_late(0)
        fetch_late(1)
        store_page(1, 0)
        scatter(1, 2, half_row(2, 1), BANK, S)
        fetch_late(2)
        round_chunk(0, 0, nc.scalar.copy)
        round_chunk(0, 1, nc.scalar.copy)
        weave_x(0, PACK, relay)
        round_chunk(0, 2, nc.scalar.copy)
        round_chunk(0, 3, nc.scalar.copy)
        regroup(1, 0, 0)
        regroup(1, 1, 0)
        store_page(1, 1)
        regroup(1, 2, 0)
        store_page(1, 2)
        for t in range(3):
            regroup(1, t, 1)
        quantize_chunk(0, 0)
        quantize_chunk(0, 1)
        quantize_x(0)
        score_pass(0)
        quantize_chunk(0, 2)
        quantize_chunk(0, 3)
        store_scales(0)
        scatter(1, 3, half_row(3, 0), 0, BANK)
        for t in range(3):
            scale_x_row(1, t)
        scatter(1, 3, half_row(3, 1), BANK, S)
        weave_x(1, 3, late)
        round_three(0)
        round_three(1)

        fetch_late(3)
        store_page(1, 3)
        round_last(0)
        scale_x(1, 3, x_words[1][:, :, 3])
        round_last(1)
        nc.vector.tensor_copy(out=stages[1, 1][:, 6 * BANK : 8 * BANK], in_=pages[1, 3][:, 2 * BANK : 4 * BANK])
        quantize_chunk(1, 0)
        round_chunk(1, 2, nc.vector.tensor_copy)
        quantize_x(1)
        score_pass(1)
        quantize_chunk(1, 2)
        quantize_chunk(1, 1)
        rounded[1, 3] = rounded[1, 1]
        interleave(nc.vector.tensor_copy, rounded[1, 3][:], staged(1, 3))
        for n in range(N // P):
            y = ring.tile([P, M], F32, name=f"y{n}", tag="h_row", bufs=3, align_bytes=ALIGN)
            nc.scalar.activation(out=y[:], in_=scores[n][:], func=ACT.Square)
            nc.sync.dma_start(out=out_0[P * n : P * (n + 1), :], in_=y[:])
        quantize_chunk(1, 3)
        store_scales(1)
